import numpy as np
import ml_dtypes


def mxq(x, axis, fmt="e4m3"):
    dtype, down = {"e4m3": (ml_dtypes.float8_e4m3fn, 7), "e5m2": (ml_dtypes.float8_e5m2, 14)}[fmt]
    v = np.moveaxis(np.asarray(x, np.float32).astype(ml_dtypes.bfloat16).astype(np.float64), axis, -1)
    blocks = v.reshape(v.shape[:-1] + (-1, 32))
    amax = np.abs(blocks).max(-1, keepdims=True)
    byte = np.maximum(np.where(amax > 0, np.frexp(amax)[1] - 1 + 127, 0) - down, 1)
    scale = np.exp2(byte - 127.0)
    codes = (blocks / scale).astype(np.float32).astype(dtype).astype(np.float64)
    return np.moveaxis((codes * scale).reshape(v.shape), -1, axis)


WIDE = False


def mx_kscale(k):
    if not WIDE:
        return np.ones(k)
    levels = np.array([10, -10, 5, -5, 0])
    if k % 512:
        return np.exp2(np.random.permutation(np.resize(levels, k // 32))).repeat(32)
    a = np.empty((k // 512, 16))
    for p in range(k // 512):
        a[p, :8] = np.random.permutation(np.resize(levels, 8))
        for g in range(8):
            far = levels[np.abs(levels - a[p, g]) >= 10]
            a[p, g + 8] = far[np.random.randint(len(far))]
    return np.exp2(a.ravel()).repeat(32)


def f64(x):
    return np.asarray(x).astype(np.float64)


def striped(idx):
    return np.tile(idx.reshape(-1, 16).T, (8, 1)).astype(np.uint16)


def unstriped(offs):
    return offs[:16].T.reshape(-1).astype(np.int64)


E2M1 = np.array([0.0, 0.5, 1.0, 1.5, 2.0, 3.0, 4.0, 6.0, -0.0, -0.5, -1.0, -1.5, -2.0, -3.0, -4.0, -6.0])


def pack_weight(w, fmt):
    k, n = w.shape
    w = f64(np.asarray(w, np.float32).astype(ml_dtypes.bfloat16)).reshape(k // 32, 32, n)
    amax = np.abs(w).max(1)
    if fmt == "e4m3":
        byte = np.frexp(amax)[1] - 1 + 127 - 7
    else:
        mant, ex = np.frexp(amax / 6.0)
        byte = np.where(mant > 0.5, ex, ex - 1) + 127
    byte = np.clip(np.where(amax > 0, byte, 1), 1, 254)
    scaled = (w * np.exp2(127.0 - byte)[:, None, :]).reshape(k, n).astype(np.float32)
    by_word = np.ascontiguousarray(scaled.reshape(k // 512, 128, 4, n).transpose(0, 1, 3, 2))
    if fmt == "e4m3":
        words = by_word.astype(ml_dtypes.float8_e4m3fn).view(np.uint8)
    else:
        c = by_word.astype(ml_dtypes.float4_e2m1fn).view(np.uint8) & 0xF
        words = (c[..., 0::2] | (c[..., 1::2] << 4)).reshape(k // 512, 128, 2 * n)
    return np.ascontiguousarray(words), np.ascontiguousarray(byte.astype(np.uint8).reshape(k // 512, 16, n))


def unpack_weight(words, scales, fmt):
    g, _, n = scales.shape
    words = np.ascontiguousarray(words).reshape(g, 128, n, -1)
    if fmt == "e4m3":
        vals = words.view(ml_dtypes.float8_e4m3fn).astype(np.float64)
    else:
        nib = np.empty((g, 128, n, 4), np.uint8)
        nib[..., 0::2] = words & 0xF
        nib[..., 1::2] = words >> 4
        vals = E2M1[nib]
    vals = vals * np.repeat(np.exp2(scales.astype(np.float64) - 127.0), 8, axis=1)[..., None]
    return vals.transpose(0, 1, 3, 2).reshape(g * 512, n)


def gelu(v):
    return 0.5 * v * (1.0 + np.tanh(np.sqrt(2.0 / np.pi) * (v + 0.044715 * v**3)))


K, T, S, T2, S2, N, M = 512, 2048, 1024, 4096, 1536, 384, 384

def setup_inputs():
    n = np.random.standard_normal
    s = mx_kscale(K)[:, None]
    u = mx_kscale(S)[:, None]
    idx = np.random.permutation(T)[:S]
    idx2 = np.random.permutation(T2)[:S2]
    main = n((K, 1))
    x = (0.9 * main * np.abs(n((1, T))) + 0.5 * n((K, T))) / np.sqrt(K)
    x2 = (-0.9 * main * np.abs(n((1, T2))) + 0.5 * n((K, T2))) / np.sqrt(K)
    tab_words, tab_scales = pack_weight(x * s, "e4m3")
    tab2_words, tab2_scales = pack_weight(x2 / s, "e4m3")
    w4_words, w4_scales = pack_weight(n((S, M)) / np.sqrt(S) / u, "e2m1")
    return {
        "tab_words": tab_words, "tab_scales": tab_scales,
        "tab2_words": tab2_words, "tab2_scales": tab2_scales,
        "offs": striped(idx), "offs2": striped(idx2),
        "qa": np.square(x[:, idx]).sum(0).astype(np.float32),
        "qb": np.square(x2[:, idx2]).sum(0).astype(np.float32),
        "hw": (np.exp(0.3 * n(S)) * u[:, 0]).astype(np.float32),
        "wd": (n((S, N)) / np.sqrt(S) / u).astype(np.float32),
        "w4_words": w4_words, "w4_scales": w4_scales,
    }

def reference(tab_words, tab_scales, tab2_words, tab2_scales, offs, offs2, qa, qb, hw, wd, w4_words, w4_scales):
    v = unpack_weight(tab_words, tab_scales, "e4m3")[:, unstriped(offs)]
    v2 = unpack_weight(tab2_words, tab2_scales, "e4m3")[:, unstriped(offs2)]
    a = v.T @ v2
    r = np.sqrt(f64(qa)[:, None] + f64(qb)[None, :] - 2.0 * a)
    z = mxq(r * f64(hw)[:, None], 0, "e4m3")
    yd = mxq(f64(wd), 0, "e4m3").T @ z
    ys = unpack_weight(w4_words, w4_scales, "e2m1").T @ z
    return np.concatenate([yd, ys], axis=0)

@@ -1,0 +1,279 @@
+from contextlib import ExitStack
+
+import concourse.mybir as mybir
+from concourse.masks import make_identity
+
+K, T, S, T2, S2, N, M = 512, 2048, 1024, 4096, 1536, 384, 384
+FLOPS = 2 * K * S * S2 + 2 * S * (N + M) * S2
+
+F32 = mybir.dt.float32
+BF16 = mybir.dt.bfloat16
+I32 = mybir.dt.int32
+U32 = mybir.dt.uint32
+U16 = mybir.dt.uint16
+U8 = mybir.dt.uint8
+FP8X4 = mybir.dt.float8_e4m3fn_x4
+FP4X4 = mybir.dt.float4_e2m1fn_x4
+ALU = mybir.AluOpType
+ACT = mybir.ActivationFunctionType
+
+P = 128
+PACK = 4
+BANK = 512
+PASSES = S // (P * PACK)
+BLOCKS = S2 // BANK
+ROW_TILES = (N + M) // P
+WD_TILES = N // P
+TAB2_ROW = 4
+GROUPS = [(0, 512, (256, 512), 512), (512, 512, (512, 512), 512), (1024, 256, (256, 256), 256), (1280, 256, (256, 256), 128)]
+
+
+def load_scale_rows(engine, plane, rows, first):
+    by_row = rows.rearrange("(q r) w -> r q w", r=4)
+    for r in range(4):
+        engine.dma_start(out=plane[first + r : P : 32], in_=by_row[r])
+
+
+def tile_list_handle_patch_deform_kernel(
+    tc, tab_words, tab_scales, tab2_words, tab2_scales, offs, offs2, qa, qb, hw, wd, w4_words, w4_scales, out
+):
+    nc = tc.nc
+    with ExitStack() as ctx:
+        keep = ctx.enter_context(tc.tile_pool(name="keep", bufs=1))
+        ring = ctx.enter_context(tc.tile_pool(name="ring", bufs=3))
+        psum = ctx.enter_context(tc.psum_pool(name="psum", bufs=4))
+
+        list1 = keep.tile([P, S // 16], U16, name="list1")
+        list2 = keep.tile([P, S2 // 16], U16, name="list2")
+        tab_w = keep.tile([P, T], I32, name="tab_w", align_bytes=64)
+        tab_s = keep.tile([P, T // 4], I32, name="tab_s", align_bytes=64)
+        qb_col = keep.tile([P, BLOCKS, PACK], F32, name="qb_col", tag="late_wd0", align_bytes=64)
+        hw_col = keep.tile([P, PASSES, PACK], F32, name="hw_col", tag="late_w4w", align_bytes=64)
+        qa_col = keep.tile([P, PASSES, PACK], F32, name="qa_col", tag="late_wd1", align_bytes=64)
+        one = keep.tile([P, 1], F32, name="one", tag="late_tab2_w", align_bytes=64)
+        warm = keep.tile([P, 1], F32, name="warm", tag="late_tab2_s", align_bytes=64)
+        ident = keep.tile([P, P], F32, name="ident", tag="late_w4s", align_bytes=64)
+
+        nc.vector.memset(tab_s[:], 0)
+        nc.vector.memset(one[:], 1.0)
+        nc.scalar.activation(warm[:], one[:], ACT.Sqrt)
+        make_identity(nc, ident[:])
+
+        nc.sync.dma_start(list1[:], offs)
+        nc.sync.dma_start(out=tab_w[:], in_=tab_words[0].rearrange("p t i -> p (t i)").bitcast(I32))
+        nc.sync.dma_start(list2[:], offs2)
+        load_scale_rows(nc.sync, tab_s, tab_scales[0].bitcast(I32), 0)
+        tab2_w = keep.tile([P, T2], I32, name="tab2_w", tag="late_tab2_w", align_bytes=64)
+        nc.sync.dma_start(out=tab2_w[:], in_=tab2_words[0].rearrange("p t i -> p (t i)").bitcast(I32))
+        tab2_s = keep.tile([P, T2 // 4], I32, name="tab2_s", tag="late_tab2_s", align_bytes=64)
+        nc.vector.memset(tab2_s[:], 0)
+        load_scale_rows(nc.scalar, tab2_s, tab2_scales[0].bitcast(I32), TAB2_ROW)
+        nc.gpsimd.dma_start(out=qb_col[:], in_=qb.rearrange("(b p c) -> p b c", p=P, c=PACK))
+        nc.gpsimd.dma_start(out=hw_col[:], in_=hw.rearrange("(a p t) -> p a t", p=P, t=PACK))
+        nc.gpsimd.dma_start(out=qa_col[:], in_=qa.rearrange("(a p t) -> p a t", p=P, t=PACK))
+
+        hw2 = keep.tile([P, PASSES, PACK], F32, name="hw2")
+        hw2qa = keep.tile([P, PASSES, PACK], F32, name="hw2qa")
+        hw2m2 = keep.tile([P, PASSES, PACK], F32, name="hw2m2")
+        nc.gpsimd.tensor_tensor(hw2[:], hw_col[:], hw_col[:], ALU.mult)
+        nc.gpsimd.tensor_tensor(hw2qa[:], hw2[:], qa_col[:], ALU.mult)
+        nc.gpsimd.tensor_scalar(hw2m2[:], hw2[:], -2.0, 0.0, ALU.mult, ALU.add)
+
+        qb_bank = []
+        for b in range(BLOCKS):
+            bank = psum.tile([P, PACK, P], F32, name=f"qb_bank{b}", tag="prod")
+            for c in range(PACK):
+                nc.tensor.transpose(bank[:, c, :], qb_col[:, b, c : c + 1].to_broadcast([P, P]), ident[:])
+            qb_bank.append(bank)
+        wd_raw = []
+        for a in range(PASSES):
+            raw = keep.tile([P, PACK, N], F32, name=f"wd_raw{a}", tag=f"late_wd{a}", align_bytes=64)
+            nc.sync.dma_start(out=raw[:], in_=wd[a * 512 : (a + 1) * 512, :].rearrange("(p t) n -> p t n", t=PACK))
+            wd_raw.append(raw)
+        w4_w = keep.tile([P, PASSES, M // 2], I32, name="w4_w", tag="late_w4w", align_bytes=64)
+        nc.sync.dma_start(out=w4_w[:], in_=w4_words.bitcast(I32).rearrange("a p w -> p a w"))
+        w4_s = keep.tile([P, PASSES, M // 4], I32, name="w4_s", tag="late_w4s", align_bytes=64)
+        nc.gpsimd.memset(w4_s[:], 0)
+        w4_rows = w4_scales.bitcast(I32).rearrange("a (q r) w -> r q a w", r=4)
+        for r in range(4):
+            nc.sync.dma_start(out=w4_s[r:P:32], in_=w4_rows[r])
+
+        qb_rows = {}
+        for b in range(1, BLOCKS):
+            rows = keep.tile([P, BANK], F32, name=f"qb_rows{b}")
+            nc.scalar.copy(rows[:].rearrange("p (n c) -> p n c", c=PACK), qb_bank[b][:].rearrange("p c n -> p n c"))
+            qb_rows[b] = rows
+
+        base = {}
+
+        def make_base(b, a):
+            for t in range(PACK):
+                q = keep.tile([P, BANK], F32, name=f"base{b}{a}{t}", tag=f"base{b}{a}{t}", align_bytes=64)
+                if (b, a, t) <= (1, 1, 1):
+                    nc.scalar.activation(
+                        q[:].rearrange("p (n c) -> p n c", c=PACK),
+                        qb_bank[b][:].rearrange("p c n -> p n c"),
+                        ACT.Identity,
+                        bias=hw2qa[:, a, t : t + 1],
+                        scale=hw2[:, a, t : t + 1],
+                    )
+                else:
+                    nc.gpsimd.tensor_scalar(
+                        q[:], qb_rows[b][:], hw2[:, a, t : t + 1], hw2qa[:, a, t : t + 1], ALU.mult, ALU.add
+                    )
+                base[b, a, t] = q
+
+        wd_bf = keep.tile([P, PASSES, N, PACK], BF16, name="wd_bf", align_bytes=64)
+        for b in range(BLOCKS):
+            if b == BLOCKS - 1:
+                for a in range(PASSES):
+                    nc.gpsimd.tensor_scalar(
+                        wd_bf[:, a], wd_raw[a][:].rearrange("p t n -> p n t"), 1.0, 0.0, ALU.mult, ALU.add
+                    )
+            for a in range(PASSES):
+                make_base(b, a)
+
+        hand_w, hand_s = {}, {}
+
+        def gather_handles(a):
+            entries = list1[:, a * 32 : (a + 1) * 32]
+            words = keep.tile([P, PACK, P], U32, name=f"hand_w{a}", align_bytes=64)
+            nc.vector.tensor_copy(words[:].rearrange("p t m -> p m t"), tab_w[:].bitcast(U32).indirect(entries))
+            picked = keep.tile([P, P, PACK], U8, name=f"picked{a}", align_bytes=64)
+            nc.vector.tensor_copy(picked[:].rearrange("p m t -> p (m t)"), tab_s[:].bitcast(U8).indirect(entries))
+            scales = keep.tile([P, PACK, P], U8, name=f"hand_s{a}", align_bytes=64)
+            nc.vector.tensor_copy(scales[:], picked[:].rearrange("p m t -> p t m"))
+            hand_w[a], hand_s[a] = words, scales
+
+        vert_w, vert_s = {}, {}
+
+        def gather_vertex_scales(b):
+            tag = f"base{b - 1}03" if b else "vert_s0"
+            scales = keep.tile([P, BANK], U8, name=f"vert_s{b}", tag=tag, align_bytes=64)
+            nc.vector.tensor_copy(scales[:], tab2_s[:].bitcast(U8).indirect(list2[:, b * 32 : (b + 1) * 32]))
+            vert_s[b] = scales
+
+        def gather_vertex_words(b):
+            tag = f"base{b - 1}11" if b else "vert_w0"
+            words = keep.tile([P, BANK], U32, name=f"vert_w{b}", tag=tag, align_bytes=64)
+            nc.vector.tensor_copy(words[:], tab2_w[:].bitcast(U32).indirect(list2[:, b * 32 : (b + 1) * 32]))
+            vert_w[b] = words
+
+        wd_w = keep.tile([P, PASSES * N], U32, name="wd_w", align_bytes=64)
+        wd_s = keep.tile([P, PASSES * N], U8, name="wd_s", align_bytes=64)
+
+        def quantize_wd():
+            flat = wd_bf[:].rearrange("p a n t -> p (a n t)")
+            for c0, c1 in ((0, 256), (256, 768)):
+                nc.vector.quantize_mx(
+                    out=wd_w[:, c0:c1].bitcast(FP8X4), scales=wd_s[:, c0:c1], in_=flat[:, 4 * c0 : 4 * c1]
+                )
+
+        def weighted_distances(group, a):
+            j0, width, chunks, unit = group
+            chunk = chunks[a]
+            b, first = divmod(j0, BANK)
+            per_bank = BANK // chunk
+            piece = min(chunk, unit)
+            square = ring.tile([P, PACK, width], F32, name="square")
+            z_bf = [
+                ring.tile([P, unit, PACK], BF16, name="z_bf", align_bytes=64, bufs=4) for u in range(width // unit)
+            ]
+            for c0 in range(0, width, chunk):
+                cols = slice(first + c0, first + c0 + chunk)
+                for t in range(PACK):
+                    if t % per_bank == 0:
+                        dots = psum.tile([P, per_bank, chunk], F32, name="dots")
+                    nc.tensor.matmul_mx(
+                        out=dots[:, t % per_bank, :],
+                        lhsT=hand_w[a][:, t, :].bitcast(FP8X4),
+                        lhsT_scale=hand_s[a][:, t, :],
+                        rhs=vert_w[b][:, cols].bitcast(FP8X4),
+                        rhs_scale=vert_s[b][TAB2_ROW:P, cols],
+                        start=True,
+                        stop=True,
+                    )
+                    nc.vector.scalar_tensor_tensor(
+                        square[:, t, c0 : c0 + chunk],
+                        dots[:, t % per_bank, :],
+                        hw2m2[:, a, t : t + 1],
+                        base[b, a, t][:, cols],
+                        ALU.mult,
+                        ALU.add,
+                    )
+                for p0 in range(c0, c0 + chunk, piece):
+                    u, u0 = divmod(p0, unit)
+                    nc.scalar.activation(
+                        z_bf[u][:, u0 : u0 + piece, :].rearrange("p (c i) t -> p c t i", i=4),
+                        square[:, :, p0 : p0 + piece].rearrange("p t (c i) -> p c t i", i=4),
+                        ACT.Sqrt,
+                    )
+            return z_bf
+
+        def quantize_z(z_bf, width):
+            z_w = ring.tile([P, width], U32, name="z_w", align_bytes=64, bufs=6)
+            z_s = ring.tile([P, width], U8, name="z_s", align_bytes=64, bufs=6)
+            nc.vector.quantize_mx(out=z_w[:].bitcast(FP8X4), scales=z_s[:], in_=z_bf[:].rearrange("p j t -> p (j t)"))
+            return z_w, z_s
+
+        def displace(j0, width, z_parts, last):
+            per_bank = min(BANK // width, WD_TILES)
+            order = list(range(WD_TILES, ROW_TILES)) + list(range(WD_TILES))
+            if per_bank > 1:
+                order = list(range(ROW_TILES))
+            for g0 in range(0, ROW_TILES, per_bank):
+                bank = psum.tile([P, per_bank, width], F32, name="prod", tag="prod")
+                for g in range(per_bank):
+                    nt = order[g0 + g]
+                    step = width if (nt < WD_TILES or width == BANK) else P
+                    for c0 in range(0, width, step):
+                        for a in range(PASSES):
+                            z_w, z_s = z_parts[a]
+                            if nt < WD_TILES:
+                                cols = slice(a * N + nt * P, a * N + (nt + 1) * P)
+                                lhs, lhs_s = wd_w[:, cols].bitcast(FP8X4), wd_s[:, cols]
+                            else:
+                                m = nt - WD_TILES
+                                lhs = w4_w[:, a, m * 64 : (m + 1) * 64].bitcast(U8).bitcast(FP4X4)
+                                lhs_s = w4_s[:, a, m * 32 : (m + 1) * 32].bitcast(U8)
+                            nc.tensor.matmul_mx(
+                                out=bank[:, g, c0 : c0 + step],
+                                lhsT=lhs,
+                                lhsT_scale=lhs_s,
+                                rhs=z_w[:, c0 : c0 + step].bitcast(FP8X4),
+                                rhs_scale=z_s[:, c0 : c0 + step],
+                                start=(a == 0),
+                                stop=(a == PASSES - 1),
+                            )
+                staged = ring.tile([P, per_bank, width], F32, name="staged", bufs=6)
+                if last and (g0 // per_bank) % 2 == 1:
+                    nc.vector.tensor_copy(staged[:], bank[:])
+                else:
+                    nc.scalar.copy(staged[:], bank[:])
+                r0 = order[g0] * P
+                nc.sync.dma_start(
+                    out=out[r0 : r0 + per_bank * P, j0 : j0 + width].rearrange("(g p) j -> p g j", p=P), in_=staged[:]
+                )
+
+        steps = [(group, a) for group in GROUPS for a in range(PASSES)]
+        gather_handles(0)
+        gather_vertex_scales(0)
+        gather_vertex_words(0)
+        made, parts = [], {}
+        for s in range(len(steps) + 1):
+            if s < len(steps):
+                made.append(weighted_distances(*steps[s]))
+                if s == 0:
+                    gather_handles(1)
+                if s in (0, 2):
+                    gather_vertex_scales(s // 2 + 1)
+                if s in (1, 3):
+                    gather_vertex_words(s // 2 + 1)
+                if s == 1:
+                    quantize_wd()
+            if s >= 1:
+                (j0, width, chunks, unit), a = steps[s - 1]
+                for u, z_bf in enumerate(made[s - 1]):
+                    parts[u, a] = quantize_z(z_bf, unit)
+                    if a == PASSES - 1:
+                        displace(j0 + u * unit, unit, [parts[u, 0], parts[u, 1]], unit == P)

@@ -1,7 +1,6 @@
 from contextlib import ExitStack
 
 import concourse.mybir as mybir
-from concourse.masks import make_identity
 
 K, T, S, T2, S2, N, M = 512, 2048, 1024, 4096, 1536, 384, 384
 FLOPS = 2 * K * S * S2 + 2 * S * (N + M) * S2
@@ -25,7 +24,8 @@ BLOCKS = S2 // BANK
 ROW_TILES = (N + M) // P
 WD_TILES = N // P
 TAB2_ROW = 4
-GROUPS = [(0, 512, (256, 512), 512), (512, 512, (512, 512), 512), (1024, 256, (256, 256), 256), (1280, 256, (256, 256), 128)]
+LAST_UNITS = [(0, 256), (256, 128), (384, 128)]
+POOL_BASES = 8
 
 
 def load_scale_rows(engine, plane, rows, first):
@@ -45,30 +45,40 @@ def tile_list_handle_patch_deform_kernel(
 
         list1 = keep.tile([P, S // 16], U16, name="list1")
         list2 = keep.tile([P, S2 // 16], U16, name="list2")
-        tab_w = keep.tile([P, T], I32, name="tab_w", align_bytes=64)
         tab_s = keep.tile([P, T // 4], I32, name="tab_s", align_bytes=64)
         qb_col = keep.tile([P, BLOCKS, PACK], F32, name="qb_col", tag="late_wd0", align_bytes=64)
         hw_col = keep.tile([P, PASSES, PACK], F32, name="hw_col", tag="late_w4w", align_bytes=64)
         qa_col = keep.tile([P, PASSES, PACK], F32, name="qa_col", tag="late_wd1", align_bytes=64)
+        tab2_s = keep.tile([P, T2 // 4], I32, name="tab2_s", align_bytes=64)
         one = keep.tile([P, 1], F32, name="one", tag="late_tab2_w", align_bytes=64)
-        warm = keep.tile([P, 1], F32, name="warm", tag="late_tab2_s", align_bytes=64)
+        zeros = keep.tile([P, P], F32, name="zeros", tag="late_tab_w", align_bytes=64)
+        warm = keep.tile([P, 1], F32, name="warm")
         ident = keep.tile([P, P], F32, name="ident", tag="late_w4s", align_bytes=64)
 
         nc.vector.memset(tab_s[:], 0)
+        nc.vector.memset(zeros[:], 0.0)
         nc.vector.memset(one[:], 1.0)
+        nc.vector.memset(tab2_s[:], 0)
         nc.scalar.activation(warm[:], one[:], ACT.Sqrt)
-        make_identity(nc, ident[:])
+        nc.gpsimd.dma_start(out=qb_col[:], in_=qb.rearrange("(b p c) -> p b c", p=P, c=PACK))
+        nc.gpsimd.affine_select(
+            out=ident[:],
+            in_=zeros[:],
+            compare_op=ALU.not_equal,
+            fill=1.0,
+            base=0,
+            pattern=[[-1, P]],
+            channel_multiplier=1,
+        )
 
         nc.sync.dma_start(list1[:], offs)
-        nc.sync.dma_start(out=tab_w[:], in_=tab_words[0].rearrange("p t i -> p (t i)").bitcast(I32))
         nc.sync.dma_start(list2[:], offs2)
         load_scale_rows(nc.sync, tab_s, tab_scales[0].bitcast(I32), 0)
+        tab_w = keep.tile([P, T], I32, name="tab_w", tag="late_tab_w", align_bytes=64)
+        nc.sync.dma_start(out=tab_w[:], in_=tab_words[0].rearrange("p t i -> p (t i)").bitcast(I32))
+        load_scale_rows(nc.sync, tab2_s, tab2_scales[0].bitcast(I32), TAB2_ROW)
         tab2_w = keep.tile([P, T2], I32, name="tab2_w", tag="late_tab2_w", align_bytes=64)
         nc.sync.dma_start(out=tab2_w[:], in_=tab2_words[0].rearrange("p t i -> p (t i)").bitcast(I32))
-        tab2_s = keep.tile([P, T2 // 4], I32, name="tab2_s", tag="late_tab2_s", align_bytes=64)
-        nc.vector.memset(tab2_s[:], 0)
-        load_scale_rows(nc.scalar, tab2_s, tab2_scales[0].bitcast(I32), TAB2_ROW)
-        nc.gpsimd.dma_start(out=qb_col[:], in_=qb.rearrange("(b p c) -> p b c", p=P, c=PACK))
         nc.gpsimd.dma_start(out=hw_col[:], in_=hw.rearrange("(a p t) -> p a t", p=P, t=PACK))
         nc.gpsimd.dma_start(out=qa_col[:], in_=qa.rearrange("(a p t) -> p a t", p=P, t=PACK))
 
@@ -98,18 +108,29 @@ def tile_list_handle_patch_deform_kernel(
         for r in range(4):
             nc.sync.dma_start(out=w4_s[r:P:32], in_=w4_rows[r])
 
-        qb_rows = {}
-        for b in range(1, BLOCKS):
-            rows = keep.tile([P, BANK], F32, name=f"qb_rows{b}")
-            nc.scalar.copy(rows[:].rearrange("p (n c) -> p n c", c=PACK), qb_bank[b][:].rearrange("p c n -> p n c"))
-            qb_rows[b] = rows
+        wd_bf = keep.tile([P, PASSES, N, PACK], BF16, name="wd_bf", align_bytes=64)
+        for a in range(PASSES):
+            for n0 in range(0, N, N // 2):
+                nc.gpsimd.tensor_scalar(
+                    wd_bf[:, a, n0 : n0 + N // 2, :],
+                    wd_raw[a][:, :, n0 : n0 + N // 2].rearrange("p t n -> p n t"),
+                    1.0,
+                    0.0,
+                    ALU.mult,
+                    ALU.add,
+                )
 
         base = {}
+        qb_rows = keep.tile([P, BANK], F32, name="qb_rows")
 
         def make_base(b, a):
             for t in range(PACK):
                 q = keep.tile([P, BANK], F32, name=f"base{b}{a}{t}", tag=f"base{b}{a}{t}", align_bytes=64)
-                if (b, a, t) <= (1, 1, 1):
+                if (b * PASSES + a) * PACK + t >= BLOCKS * PASSES * PACK - POOL_BASES:
+                    nc.gpsimd.tensor_scalar(
+                        q[:], qb_rows[:], hw2[:, a, t : t + 1], hw2qa[:, a, t : t + 1], ALU.mult, ALU.add
+                    )
+                else:
                     nc.scalar.activation(
                         q[:].rearrange("p (n c) -> p n c", c=PACK),
                         qb_bank[b][:].rearrange("p c n -> p n c"),
@@ -117,163 +138,172 @@ def tile_list_handle_patch_deform_kernel(
                         bias=hw2qa[:, a, t : t + 1],
                         scale=hw2[:, a, t : t + 1],
                     )
-                else:
-                    nc.gpsimd.tensor_scalar(
-                        q[:], qb_rows[b][:], hw2[:, a, t : t + 1], hw2qa[:, a, t : t + 1], ALU.mult, ALU.add
-                    )
                 base[b, a, t] = q
-
-        wd_bf = keep.tile([P, PASSES, N, PACK], BF16, name="wd_bf", align_bytes=64)
-        for b in range(BLOCKS):
-            if b == BLOCKS - 1:
-                for a in range(PASSES):
-                    nc.gpsimd.tensor_scalar(
-                        wd_bf[:, a], wd_raw[a][:].rearrange("p t n -> p n t"), 1.0, 0.0, ALU.mult, ALU.add
-                    )
-            for a in range(PASSES):
-                make_base(b, a)
 
         hand_w, hand_s = {}, {}
 
         def gather_handles(a):
             entries = list1[:, a * 32 : (a + 1) * 32]
-            words = keep.tile([P, PACK, P], U32, name=f"hand_w{a}", align_bytes=64)
-            nc.vector.tensor_copy(words[:].rearrange("p t m -> p m t"), tab_w[:].bitcast(U32).indirect(entries))
-            picked = keep.tile([P, P, PACK], U8, name=f"picked{a}", align_bytes=64)
+            picked = keep.tile([P, P, PACK], U8, name=f"picked{a}", tag=f"picked{a}", align_bytes=64)
             nc.vector.tensor_copy(picked[:].rearrange("p m t -> p (m t)"), tab_s[:].bitcast(U8).indirect(entries))
             scales = keep.tile([P, PACK, P], U8, name=f"hand_s{a}", align_bytes=64)
             nc.vector.tensor_copy(scales[:], picked[:].rearrange("p m t -> p t m"))
+            words = keep.tile([P, PACK, P], U32, name=f"hand_w{a}", align_bytes=64)
+            nc.vector.tensor_copy(words[:].rearrange("p t m -> p m t"), tab_w[:].bitcast(U32).indirect(entries))
             hand_w[a], hand_s[a] = words, scales
 
         vert_w, vert_s = {}, {}
 
         def gather_vertex_scales(b):
-            tag = f"base{b - 1}03" if b else "vert_s0"
-            scales = keep.tile([P, BANK], U8, name=f"vert_s{b}", tag=tag, align_bytes=64)
+            scales = keep.tile([P, BANK], U8, name=f"vert_s{b}", align_bytes=64)
             nc.vector.tensor_copy(scales[:], tab2_s[:].bitcast(U8).indirect(list2[:, b * 32 : (b + 1) * 32]))
             vert_s[b] = scales
 
         def gather_vertex_words(b):
-            tag = f"base{b - 1}11" if b else "vert_w0"
+            tag = f"base{b - 1}12" if b else "vert_w0"
             words = keep.tile([P, BANK], U32, name=f"vert_w{b}", tag=tag, align_bytes=64)
             nc.vector.tensor_copy(words[:], tab2_w[:].bitcast(U32).indirect(list2[:, b * 32 : (b + 1) * 32]))
             vert_w[b] = words
 
-        wd_w = keep.tile([P, PASSES * N], U32, name="wd_w", align_bytes=64)
-        wd_s = keep.tile([P, PASSES * N], U8, name="wd_s", align_bytes=64)
+        wd_q = {}
 
         def quantize_wd():
+            wd_w = keep.tile([P, PASSES * N], U32, name="wd_w", tag="base013", align_bytes=64)
+            wd_s = keep.tile([P, PASSES * N], U8, name="wd_s", align_bytes=64)
             flat = wd_bf[:].rearrange("p a n t -> p (a n t)")
             for c0, c1 in ((0, 256), (256, 768)):
                 nc.vector.quantize_mx(
                     out=wd_w[:, c0:c1].bitcast(FP8X4), scales=wd_s[:, c0:c1], in_=flat[:, 4 * c0 : 4 * c1]
                 )
+            wd_q["words"], wd_q["scales"] = wd_w, wd_s
 
-        def weighted_distances(group, a):
-            j0, width, chunks, unit = group
-            chunk = chunks[a]
-            b, first = divmod(j0, BANK)
-            per_bank = BANK // chunk
-            piece = min(chunk, unit)
-            square = ring.tile([P, PACK, width], F32, name="square")
-            z_bf = [
-                ring.tile([P, unit, PACK], BF16, name="z_bf", align_bytes=64, bufs=4) for u in range(width // unit)
-            ]
-            for c0 in range(0, width, chunk):
-                cols = slice(first + c0, first + c0 + chunk)
-                for t in range(PACK):
-                    if t % per_bank == 0:
-                        dots = psum.tile([P, per_bank, chunk], F32, name="dots")
-                    nc.tensor.matmul_mx(
-                        out=dots[:, t % per_bank, :],
-                        lhsT=hand_w[a][:, t, :].bitcast(FP8X4),
-                        lhsT_scale=hand_s[a][:, t, :],
-                        rhs=vert_w[b][:, cols].bitcast(FP8X4),
-                        rhs_scale=vert_s[b][TAB2_ROW:P, cols],
-                        start=True,
-                        stop=True,
-                    )
-                    nc.vector.scalar_tensor_tensor(
-                        square[:, t, c0 : c0 + chunk],
-                        dots[:, t % per_bank, :],
-                        hw2m2[:, a, t : t + 1],
-                        base[b, a, t][:, cols],
-                        ALU.mult,
-                        ALU.add,
-                    )
-                for p0 in range(c0, c0 + chunk, piece):
-                    u, u0 = divmod(p0, unit)
-                    nc.scalar.activation(
-                        z_bf[u][:, u0 : u0 + piece, :].rearrange("p (c i) t -> p c t i", i=4),
-                        square[:, :, p0 : p0 + piece].rearrange("p t (c i) -> p c t i", i=4),
-                        ACT.Sqrt,
-                    )
-            return z_bf
+        square, z_bf, z_w, z_s = {}, {}, {}, {}
 
-        def quantize_z(z_bf, width):
-            z_w = ring.tile([P, width], U32, name="z_w", align_bytes=64, bufs=6)
-            z_s = ring.tile([P, width], U8, name="z_s", align_bytes=64, bufs=6)
-            nc.vector.quantize_mx(out=z_w[:].bitcast(FP8X4), scales=z_s[:], in_=z_bf[:].rearrange("p j t -> p (j t)"))
-            return z_w, z_s
-
-        def displace(j0, width, z_parts, last):
-            per_bank = min(BANK // width, WD_TILES)
-            order = list(range(WD_TILES, ROW_TILES)) + list(range(WD_TILES))
-            if per_bank > 1:
-                order = list(range(ROW_TILES))
-            for g0 in range(0, ROW_TILES, per_bank):
-                bank = psum.tile([P, per_bank, width], F32, name="prod", tag="prod")
-                for g in range(per_bank):
-                    nt = order[g0 + g]
-                    step = width if (nt < WD_TILES or width == BANK) else P
-                    for c0 in range(0, width, step):
-                        for a in range(PASSES):
-                            z_w, z_s = z_parts[a]
-                            if nt < WD_TILES:
-                                cols = slice(a * N + nt * P, a * N + (nt + 1) * P)
-                                lhs, lhs_s = wd_w[:, cols].bitcast(FP8X4), wd_s[:, cols]
-                            else:
-                                m = nt - WD_TILES
-                                lhs = w4_w[:, a, m * 64 : (m + 1) * 64].bitcast(U8).bitcast(FP4X4)
-                                lhs_s = w4_s[:, a, m * 32 : (m + 1) * 32].bitcast(U8)
-                            nc.tensor.matmul_mx(
-                                out=bank[:, g, c0 : c0 + step],
-                                lhsT=lhs,
-                                lhsT_scale=lhs_s,
-                                rhs=z_w[:, c0 : c0 + step].bitcast(FP8X4),
-                                rhs_scale=z_s[:, c0 : c0 + step],
-                                start=(a == 0),
-                                stop=(a == PASSES - 1),
-                            )
-                staged = ring.tile([P, per_bank, width], F32, name="staged", bufs=6)
-                if last and (g0 // per_bank) % 2 == 1:
-                    nc.vector.tensor_copy(staged[:], bank[:])
-                else:
-                    nc.scalar.copy(staged[:], bank[:])
-                r0 = order[g0] * P
-                nc.sync.dma_start(
-                    out=out[r0 : r0 + per_bank * P, j0 : j0 + width].rearrange("(g p) j -> p g j", p=P), in_=staged[:]
+        def squares(b, a, c0, width):
+            if c0 == 0:
+                square[b, a] = ring.tile([P, PACK, BANK], F32, name="square")
+                z_bf[b, a] = ring.tile([P, BANK, PACK], BF16, name="z_bf", align_bytes=64)
+                z_w[b, a] = ring.tile([P, BANK], U32, name="z_w", align_bytes=64, bufs=4)
+                z_s[b, a] = ring.tile([P, BANK], U8, name="z_s", align_bytes=64, bufs=4)
+            per_bank = BANK // width
+            cols = slice(c0, c0 + width)
+            for t in range(PACK):
+                if t % per_bank == 0:
+                    dots = psum.tile([P, per_bank, width], F32, name="dots")
+                nc.tensor.matmul_mx(
+                    out=dots[:, t % per_bank, :],
+                    lhsT=hand_w[a][:, t, :].bitcast(FP8X4),
+                    lhsT_scale=hand_s[a][:, t, :],
+                    rhs=vert_w[b][:, cols].bitcast(FP8X4),
+                    rhs_scale=vert_s[b][TAB2_ROW:P, cols],
+                    start=True,
+                    stop=True,
+                )
+                nc.vector.scalar_tensor_tensor(
+                    square[b, a][:, t, cols],
+                    dots[:, t % per_bank, :],
+                    hw2m2[:, a, t : t + 1],
+                    base[b, a, t][:, cols],
+                    ALU.mult,
+                    ALU.add,
                 )
 
-        steps = [(group, a) for group in GROUPS for a in range(PASSES)]
+        def roots(b, a, c0, width):
+            nc.scalar.activation(
+                z_bf[b, a][:, c0 : c0 + width, :].rearrange("p (c i) t -> p c t i", i=4),
+                square[b, a][:, :, c0 : c0 + width].rearrange("p t (c i) -> p c t i", i=4),
+                ACT.Sqrt,
+            )
+
+        def quantize_z(b, a, c0, width):
+            cols = slice(c0, c0 + width)
+            nc.vector.quantize_mx(
+                out=z_w[b, a][:, cols].bitcast(FP8X4),
+                scales=z_s[b, a][:, cols],
+                in_=z_bf[b, a][:, cols, :].rearrange("p j t -> p (j t)"),
+            )
+
+        def displace(b, first, width, g0, on_vector):
+            per_bank = min(BANK // width, WD_TILES)
+            bank = psum.tile([P, per_bank, width], F32, name="prod", tag="prod")
+            for g in range(per_bank):
+                nt = g0 + g
+                step = width if (nt < WD_TILES or width == BANK) else P
+                for c0 in range(0, width, step):
+                    cols = slice(first + c0, first + c0 + step)
+                    for a in range(PASSES):
+                        if nt < WD_TILES:
+                            rows = slice(a * N + nt * P, a * N + (nt + 1) * P)
+                            lhs, lhs_s = wd_q["words"][:, rows].bitcast(FP8X4), wd_q["scales"][:, rows]
+                        else:
+                            m = nt - WD_TILES
+                            lhs = w4_w[:, a, m * 64 : (m + 1) * 64].bitcast(U8).bitcast(FP4X4)
+                            lhs_s = w4_s[:, a, m * 32 : (m + 1) * 32].bitcast(U8)
+                        nc.tensor.matmul_mx(
+                            out=bank[:, g, c0 : c0 + step],
+                            lhsT=lhs,
+                            lhsT_scale=lhs_s,
+                            rhs=z_w[b, a][:, cols].bitcast(FP8X4),
+                            rhs_scale=z_s[b, a][:, cols],
+                            start=(a == 0),
+                            stop=(a == PASSES - 1),
+                        )
+            staged = ring.tile([P, per_bank, width], F32, name="staged", bufs=8)
+            if on_vector:
+                nc.vector.tensor_copy(staged[:], bank[:])
+            else:
+                nc.scalar.copy(staged[:], bank[:])
+            j0 = b * BANK + first
+            nc.sync.dma_start(
+                out=out[g0 * P : (g0 + per_bank) * P, j0 : j0 + width].rearrange("(g p) j -> p g j", p=P),
+                in_=staged[:],
+            )
+
+        def whole_step(b, a):
+            squares(b, a, 0, BANK)
+            roots(b, a, 0, BANK)
+
+        make_base(0, 0)
+        make_base(0, 1)
         gather_handles(0)
         gather_vertex_scales(0)
         gather_vertex_words(0)
-        made, parts = [], {}
-        for s in range(len(steps) + 1):
-            if s < len(steps):
-                made.append(weighted_distances(*steps[s]))
-                if s == 0:
-                    gather_handles(1)
-                if s in (0, 2):
-                    gather_vertex_scales(s // 2 + 1)
-                if s in (1, 3):
-                    gather_vertex_words(s // 2 + 1)
-                if s == 1:
-                    quantize_wd()
-            if s >= 1:
-                (j0, width, chunks, unit), a = steps[s - 1]
-                for u, z_bf in enumerate(made[s - 1]):
-                    parts[u, a] = quantize_z(z_bf, unit)
-                    if a == PASSES - 1:
-                        displace(j0 + u * unit, unit, [parts[u, 0], parts[u, 1]], unit == P)
+        whole_step(0, 0)
+        gather_handles(1)
+        whole_step(0, 1)
+        gather_vertex_scales(1)
+        gather_vertex_scales(2)
+        quantize_z(0, 0, 0, BANK)
+        gather_vertex_words(1)
+        quantize_wd()
+        quantize_z(0, 1, 0, BANK)
+
+        make_base(1, 0)
+        make_base(1, 1)
+        nc.scalar.copy(qb_rows[:].rearrange("p (n c) -> p n c", c=PACK), qb_bank[2][:].rearrange("p c n -> p n c"))
+        whole_step(1, 0)
+        whole_step(1, 1)
+        quantize_z(1, 0, 0, BANK)
+        gather_vertex_words(2)
+        quantize_z(1, 1, 0, BANK)
+        for nt in range(ROW_TILES):
+            displace(0, 0, BANK, nt, False)
+
+        make_base(2, 0)
+        make_base(2, 1)
+        whole_step(2, 0)
+        for nt in range(5):
+            displace(1, 0, BANK, nt, False)
+        squares(2, 1, 0, 256)
+        roots(2, 1, 0, 256)
+        squares(2, 1, 256, 256)
+        roots(2, 1, 256, 128)
+        roots(2, 1, 384, 128)
+        quantize_z(2, 0, 0, BANK)
+        for nt in range(5, ROW_TILES):
+            displace(1, 0, BANK, nt, True)
+        for first, width in LAST_UNITS:
+            quantize_z(2, 1, first, width)
+            per_bank = min(BANK // width, WD_TILES)
+            for g0 in range(0, ROW_TILES, per_bank):
+                displace(2, first, width, g0, (g0 // per_bank) % 2 == 1)

@@ -19,19 +19,25 @@ ACT = mybir.ActivationFunctionType
 P = 128
 PACK = 4
 BANK = 512
+HALF = BANK // 2
 PASSES = S // (P * PACK)
 BLOCKS = S2 // BANK
+LAST = BLOCKS - 1
+LIST_COLS = BANK // 16
 ROW_TILES = (N + M) // P
 WD_TILES = N // P
+LINE = 4
 TAB2_ROW = 4
-LAST_UNITS = [(0, 256), (256, 128), (384, 128)]
-POOL_BASES = 8
+LAST_PIECES = [(0, HALF), (HALF, P), (HALF + P, P)]
+PSUM_BUFS = 4
+RING_BUFS = 3
+Z_BUFS = 4
+STAGED_BUFS = 8
 
 
-def load_scale_rows(engine, plane, rows, first):
-    by_row = rows.rearrange("(q r) w -> r q w", r=4)
+def load_scale_rows(nc, tile, rows, first):
     for r in range(4):
-        engine.dma_start(out=plane[first + r : P : 32], in_=by_row[r])
+        nc.sync.dma_start(out=tile[first + r : P : 32], in_=rows[r])
 
 
 def tile_list_handle_patch_deform_kernel(
@@ -40,27 +46,25 @@ def tile_list_handle_patch_deform_kernel(
     nc = tc.nc
     with ExitStack() as ctx:
         keep = ctx.enter_context(tc.tile_pool(name="keep", bufs=1))
-        ring = ctx.enter_context(tc.tile_pool(name="ring", bufs=3))
-        psum = ctx.enter_context(tc.psum_pool(name="psum", bufs=4))
+        ring = ctx.enter_context(tc.tile_pool(name="ring", bufs=RING_BUFS))
+        psum = ctx.enter_context(tc.psum_pool(name="psum", bufs=PSUM_BUFS))
 
         list1 = keep.tile([P, S // 16], U16, name="list1")
         list2 = keep.tile([P, S2 // 16], U16, name="list2")
         tab_s = keep.tile([P, T // 4], I32, name="tab_s", align_bytes=64)
-        qb_col = keep.tile([P, BLOCKS, PACK], F32, name="qb_col", tag="late_wd0", align_bytes=64)
-        hw_col = keep.tile([P, PASSES, PACK], F32, name="hw_col", tag="late_w4w", align_bytes=64)
-        qa_col = keep.tile([P, PASSES, PACK], F32, name="qa_col", tag="late_wd1", align_bytes=64)
+        qb_col = keep.tile([P, BLOCKS, PACK], F32, name="qb_col", tag="after_qb", align_bytes=64)
+        hw_col = keep.tile([P, PASSES, PACK], F32, name="hw_col", tag="after_hw", align_bytes=64)
+        qa_col = keep.tile([P, PASSES, PACK], F32, name="qa_col", tag="after_qa", align_bytes=64)
         tab2_s = keep.tile([P, T2 // 4], I32, name="tab2_s", align_bytes=64)
-        one = keep.tile([P, 1], F32, name="one", tag="late_tab2_w", align_bytes=64)
-        zeros = keep.tile([P, P], F32, name="zeros", tag="late_tab_w", align_bytes=64)
-        warm = keep.tile([P, 1], F32, name="warm")
-        ident = keep.tile([P, P], F32, name="ident", tag="late_w4s", align_bytes=64)
+        zeros = keep.tile([P, P], F32, name="zeros", tag="after_zeros", align_bytes=64)
+        ident = keep.tile([P, P], F32, name="ident", tag="after_ident", align_bytes=64)
 
         nc.vector.memset(tab_s[:], 0)
         nc.vector.memset(zeros[:], 0.0)
-        nc.vector.memset(one[:], 1.0)
         nc.vector.memset(tab2_s[:], 0)
-        nc.scalar.activation(warm[:], one[:], ACT.Sqrt)
-        nc.gpsimd.dma_start(out=qb_col[:], in_=qb.rearrange("(b p c) -> p b c", p=P, c=PACK))
+        nc.scalar.dma_start(out=qb_col[:], in_=qb.rearrange("(b p c) -> p b c", p=P, c=PACK))
+        nc.gpsimd.dma_start(out=qa_col[:], in_=qa.rearrange("(a p t) -> p a t", p=P, t=PACK))
+        nc.gpsimd.dma_start(out=hw_col[:], in_=hw.rearrange("(a p t) -> p a t", p=P, t=PACK))
         nc.gpsimd.affine_select(
             out=ident[:],
             in_=zeros[:],
@@ -73,147 +77,139 @@ def tile_list_handle_patch_deform_kernel(
 
         nc.sync.dma_start(list1[:], offs)
         nc.sync.dma_start(list2[:], offs2)
-        load_scale_rows(nc.sync, tab_s, tab_scales[0].bitcast(I32), 0)
-        tab_w = keep.tile([P, T], I32, name="tab_w", tag="late_tab_w", align_bytes=64)
+        load_scale_rows(nc, tab_s, tab_scales[0].bitcast(I32).rearrange("(q r) w -> r q w", r=4), 0)
+        tab_w = keep.tile([P, T], I32, name="tab_w", tag="after_zeros", align_bytes=64)
         nc.sync.dma_start(out=tab_w[:], in_=tab_words[0].rearrange("p t i -> p (t i)").bitcast(I32))
-        load_scale_rows(nc.sync, tab2_s, tab2_scales[0].bitcast(I32), TAB2_ROW)
-        tab2_w = keep.tile([P, T2], I32, name="tab2_w", tag="late_tab2_w", align_bytes=64)
-        nc.sync.dma_start(out=tab2_w[:], in_=tab2_words[0].rearrange("p t i -> p (t i)").bitcast(I32))
-        nc.gpsimd.dma_start(out=hw_col[:], in_=hw.rearrange("(a p t) -> p a t", p=P, t=PACK))
-        nc.gpsimd.dma_start(out=qa_col[:], in_=qa.rearrange("(a p t) -> p a t", p=P, t=PACK))
+        load_scale_rows(nc, tab2_s, tab2_scales[0].bitcast(I32).rearrange("(q r) w -> r q w", r=4), TAB2_ROW)
 
         hw2 = keep.tile([P, PASSES, PACK], F32, name="hw2")
-        hw2qa = keep.tile([P, PASSES, PACK], F32, name="hw2qa")
-        hw2m2 = keep.tile([P, PASSES, PACK], F32, name="hw2m2")
+        hw2_qa = keep.tile([P, PASSES, PACK], F32, name="hw2_qa")
+        hw2_m2 = keep.tile([P, PASSES, PACK], F32, name="hw2_m2")
         nc.gpsimd.tensor_tensor(hw2[:], hw_col[:], hw_col[:], ALU.mult)
-        nc.gpsimd.tensor_tensor(hw2qa[:], hw2[:], qa_col[:], ALU.mult)
-        nc.gpsimd.tensor_scalar(hw2m2[:], hw2[:], -2.0, 0.0, ALU.mult, ALU.add)
+        nc.gpsimd.tensor_tensor(hw2_qa[:], hw2[:], qa_col[:], ALU.mult)
+        hw_m2 = keep.tile([P, PASSES, PACK], F32, name="hw_m2", tag="after_hw_m2", align_bytes=64)
+        nc.gpsimd.tensor_scalar(hw_m2[:], hw_col[:], -2.0, 0.0, ALU.mult, ALU.add)
+        nc.gpsimd.tensor_tensor(hw2_m2[:], hw_m2[:], hw_col[:], ALU.mult)
+        tab2_w = keep.tile([P, T2], I32, name="tab2_w", tag="after_qa", align_bytes=64)
+        nc.sync.dma_start(out=tab2_w[:], in_=tab2_words[0].rearrange("p t i -> p (t i)").bitcast(I32))
 
         qb_bank = []
         for b in range(BLOCKS):
-            bank = psum.tile([P, PACK, P], F32, name=f"qb_bank{b}", tag="prod")
+            spread = psum.tile([P, PACK, P], F32, name=f"qb_bank{b}", tag="prod")
             for c in range(PACK):
-                nc.tensor.transpose(bank[:, c, :], qb_col[:, b, c : c + 1].to_broadcast([P, P]), ident[:])
-            qb_bank.append(bank)
+                nc.tensor.transpose(spread[:, c, :], qb_col[:, b, c : c + 1].to_broadcast([P, P]), ident[:])
+            qb_bank.append(spread)
+
         wd_raw = []
-        for a in range(PASSES):
-            raw = keep.tile([P, PACK, N], F32, name=f"wd_raw{a}", tag=f"late_wd{a}", align_bytes=64)
-            nc.sync.dma_start(out=raw[:], in_=wd[a * 512 : (a + 1) * 512, :].rearrange("(p t) n -> p t n", t=PACK))
+        for a, slot in enumerate(("after_hw", "after_hw_m2")):
+            raw = keep.tile([P, PACK, N], F32, name=f"wd_raw{a}", tag=slot, align_bytes=64)
+            rows = wd[a * P * PACK : (a + 1) * P * PACK, :]
+            nc.sync.dma_start(out=raw[:], in_=rows.rearrange("(p t) n -> p t n", t=PACK))
             wd_raw.append(raw)
-        w4_w = keep.tile([P, PASSES, M // 2], I32, name="w4_w", tag="late_w4w", align_bytes=64)
+        w4_w = keep.tile([P, PASSES, M // 2], I32, name="w4_w", tag="after_qb", align_bytes=64)
         nc.sync.dma_start(out=w4_w[:], in_=w4_words.bitcast(I32).rearrange("a p w -> p a w"))
-        w4_s = keep.tile([P, PASSES, M // 4], I32, name="w4_s", tag="late_w4s", align_bytes=64)
+        w4_s = keep.tile([P, PASSES, M // 4], I32, name="w4_s", tag="after_ident", align_bytes=64)
         nc.gpsimd.memset(w4_s[:], 0)
-        w4_rows = w4_scales.bitcast(I32).rearrange("a (q r) w -> r q a w", r=4)
-        for r in range(4):
-            nc.sync.dma_start(out=w4_s[r:P:32], in_=w4_rows[r])
+        load_scale_rows(nc, w4_s, w4_scales.bitcast(I32).rearrange("a (q r) w -> r q a w", r=4), 0)
 
-        wd_bf = keep.tile([P, PASSES, N, PACK], BF16, name="wd_bf", align_bytes=64)
-        for a in range(PASSES):
-            for n0 in range(0, N, N // 2):
-                nc.gpsimd.tensor_scalar(
-                    wd_bf[:, a, n0 : n0 + N // 2, :],
-                    wd_raw[a][:, :, n0 : n0 + N // 2].rearrange("p t n -> p n t"),
-                    1.0,
-                    0.0,
-                    ALU.mult,
-                    ALU.add,
-                )
-
-        base = {}
-        qb_rows = keep.tile([P, BANK], F32, name="qb_rows")
+        base, hand_w, hand_s, vert_w, vert_s, wd_q = {}, {}, {}, {}, {}, {}
+        square, z_bf, z_w, z_s = {}, {}, {}, {}
 
         def make_base(b, a):
             for t in range(PACK):
-                q = keep.tile([P, BANK], F32, name=f"base{b}{a}{t}", tag=f"base{b}{a}{t}", align_bytes=64)
-                if (b * PASSES + a) * PACK + t >= BLOCKS * PASSES * PACK - POOL_BASES:
+                tile = keep.tile([P, BANK], F32, name=f"base{b}{a}{t}", tag=f"base{b}{a}{t}", align_bytes=64)
+                if b == LAST:
                     nc.gpsimd.tensor_scalar(
-                        q[:], qb_rows[:], hw2[:, a, t : t + 1], hw2qa[:, a, t : t + 1], ALU.mult, ALU.add
+                        tile[:], qb_last[:], hw2[:, a, t : t + 1], hw2_qa[:, a, t : t + 1], ALU.mult, ALU.add
                     )
                 else:
                     nc.scalar.activation(
-                        q[:].rearrange("p (n c) -> p n c", c=PACK),
+                        tile[:].rearrange("p (n c) -> p n c", c=PACK),
                         qb_bank[b][:].rearrange("p c n -> p n c"),
                         ACT.Identity,
-                        bias=hw2qa[:, a, t : t + 1],
+                        bias=hw2_qa[:, a, t : t + 1],
                         scale=hw2[:, a, t : t + 1],
                     )
-                base[b, a, t] = q
-
-        hand_w, hand_s = {}, {}
+                base[b, a, t] = tile
 
         def gather_handles(a):
-            entries = list1[:, a * 32 : (a + 1) * 32]
-            picked = keep.tile([P, P, PACK], U8, name=f"picked{a}", tag=f"picked{a}", align_bytes=64)
+            entries = list1[:, a * LIST_COLS : (a + 1) * LIST_COLS]
+            picked = keep.tile([P, P, PACK], U8, name=f"picked{a}", align_bytes=64)
             nc.vector.tensor_copy(picked[:].rearrange("p m t -> p (m t)"), tab_s[:].bitcast(U8).indirect(entries))
-            scales = keep.tile([P, PACK, P], U8, name=f"hand_s{a}", align_bytes=64)
-            nc.vector.tensor_copy(scales[:], picked[:].rearrange("p m t -> p t m"))
-            words = keep.tile([P, PACK, P], U32, name=f"hand_w{a}", align_bytes=64)
-            nc.vector.tensor_copy(words[:].rearrange("p t m -> p m t"), tab_w[:].bitcast(U32).indirect(entries))
-            hand_w[a], hand_s[a] = words, scales
-
-        vert_w, vert_s = {}, {}
+            hand_s[a] = keep.tile([P, PACK, P], U8, name=f"hand_s{a}", align_bytes=64)
+            nc.vector.tensor_copy(hand_s[a][:], picked[:].rearrange("p m t -> p t m"))
+            hand_w[a] = keep.tile([P, PACK, P], U32, name=f"hand_w{a}", align_bytes=64)
+            nc.vector.tensor_copy(hand_w[a][:].rearrange("p t m -> p m t"), tab_w[:].bitcast(U32).indirect(entries))
 
         def gather_vertex_scales(b):
-            scales = keep.tile([P, BANK], U8, name=f"vert_s{b}", align_bytes=64)
-            nc.vector.tensor_copy(scales[:], tab2_s[:].bitcast(U8).indirect(list2[:, b * 32 : (b + 1) * 32]))
-            vert_s[b] = scales
+            vert_s[b] = keep.tile([P, BANK], U8, name=f"vert_s{b}", align_bytes=64)
+            entries = list2[:, b * LIST_COLS : (b + 1) * LIST_COLS]
+            nc.vector.tensor_copy(vert_s[b][:], tab2_s[:].bitcast(U8).indirect(entries))
 
-        def gather_vertex_words(b):
-            tag = f"base{b - 1}12" if b else "vert_w0"
-            words = keep.tile([P, BANK], U32, name=f"vert_w{b}", tag=tag, align_bytes=64)
-            nc.vector.tensor_copy(words[:], tab2_w[:].bitcast(U32).indirect(list2[:, b * 32 : (b + 1) * 32]))
-            vert_w[b] = words
-
-        wd_q = {}
+        def gather_vertex_words(b, slot):
+            vert_w[b] = keep.tile([P, BANK], U32, name=f"vert_w{b}", tag=slot, align_bytes=64)
+            entries = list2[:, b * LIST_COLS : (b + 1) * LIST_COLS]
+            nc.vector.tensor_copy(vert_w[b][:], tab2_w[:].bitcast(U32).indirect(entries))
 
         def quantize_wd():
-            wd_w = keep.tile([P, PASSES * N], U32, name="wd_w", tag="base013", align_bytes=64)
-            wd_s = keep.tile([P, PASSES * N], U8, name="wd_s", align_bytes=64)
+            wd_bf = keep.tile([P, PASSES, N, PACK], BF16, name="wd_bf", align_bytes=64)
+            for a in range(PASSES):
+                for n0 in range(0, N, N // 2):
+                    nc.scalar.copy(
+                        wd_bf[:, a, n0 : n0 + N // 2, :].rearrange("p (c i) t -> p c t i", i=LINE),
+                        wd_raw[a][:, :, n0 : n0 + N // 2].rearrange("p t (c i) -> p c t i", i=LINE),
+                    )
+            wd_q["words"] = keep.tile([P, PASSES * N], U32, name="wd_w", tag="base003", align_bytes=64)
+            wd_q["scales"] = keep.tile([P, PASSES * N], U8, name="wd_s", align_bytes=64)
             flat = wd_bf[:].rearrange("p a n t -> p (a n t)")
-            for c0, c1 in ((0, 256), (256, 768)):
+            for c0, c1 in ((0, HALF), (HALF, PASSES * N)):
                 nc.vector.quantize_mx(
-                    out=wd_w[:, c0:c1].bitcast(FP8X4), scales=wd_s[:, c0:c1], in_=flat[:, 4 * c0 : 4 * c1]
+                    out=wd_q["words"][:, c0:c1].bitcast(FP8X4),
+                    scales=wd_q["scales"][:, c0:c1],
+                    in_=flat[:, PACK * c0 : PACK * c1],
                 )
-            wd_q["words"], wd_q["scales"] = wd_w, wd_s
-
-        square, z_bf, z_w, z_s = {}, {}, {}, {}
 
         def squares(b, a, c0, width):
             if c0 == 0:
                 square[b, a] = ring.tile([P, PACK, BANK], F32, name="square")
                 z_bf[b, a] = ring.tile([P, BANK, PACK], BF16, name="z_bf", align_bytes=64)
-                z_w[b, a] = ring.tile([P, BANK], U32, name="z_w", align_bytes=64, bufs=4)
-                z_s[b, a] = ring.tile([P, BANK], U8, name="z_s", align_bytes=64, bufs=4)
+                z_w[b, a] = ring.tile([P, BANK], U32, name="z_w", align_bytes=64, bufs=Z_BUFS)
+                z_s[b, a] = ring.tile([P, BANK], U8, name="z_s", align_bytes=64, bufs=Z_BUFS)
             per_bank = BANK // width
             cols = slice(c0, c0 + width)
-            for t in range(PACK):
-                if t % per_bank == 0:
-                    dots = psum.tile([P, per_bank, width], F32, name="dots")
-                nc.tensor.matmul_mx(
-                    out=dots[:, t % per_bank, :],
-                    lhsT=hand_w[a][:, t, :].bitcast(FP8X4),
-                    lhsT_scale=hand_s[a][:, t, :],
-                    rhs=vert_w[b][:, cols].bitcast(FP8X4),
-                    rhs_scale=vert_s[b][TAB2_ROW:P, cols],
-                    start=True,
-                    stop=True,
-                )
-                nc.vector.scalar_tensor_tensor(
-                    square[b, a][:, t, cols],
-                    dots[:, t % per_bank, :],
-                    hw2m2[:, a, t : t + 1],
-                    base[b, a, t][:, cols],
-                    ALU.mult,
-                    ALU.add,
-                )
+            for t0 in range(0, PACK, per_bank):
+                dots = psum.tile([P, per_bank, width], F32, name="dots")
+                for g in range(per_bank):
+                    nc.tensor.matmul_mx(
+                        out=dots[:, g, :],
+                        lhsT=hand_w[a][:, t0 + g, :].bitcast(FP8X4),
+                        lhsT_scale=hand_s[a][:, t0 + g, :],
+                        rhs=vert_w[b][:, cols].bitcast(FP8X4),
+                        rhs_scale=vert_s[b][TAB2_ROW:P, cols],
+                        start=True,
+                        stop=True,
+                    )
+                for g in range(per_bank):
+                    t = t0 + g
+                    nc.vector.scalar_tensor_tensor(
+                        square[b, a][:, t, cols],
+                        dots[:, g, :],
+                        hw2_m2[:, a, t : t + 1],
+                        base[b, a, t][:, cols],
+                        ALU.mult,
+                        ALU.add,
+                    )
 
         def roots(b, a, c0, width):
             nc.scalar.activation(
-                z_bf[b, a][:, c0 : c0 + width, :].rearrange("p (c i) t -> p c t i", i=4),
-                square[b, a][:, :, c0 : c0 + width].rearrange("p t (c i) -> p c t i", i=4),
+                z_bf[b, a][:, c0 : c0 + width, :].rearrange("p (c i) t -> p c t i", i=LINE),
+                square[b, a][:, :, c0 : c0 + width].rearrange("p t (c i) -> p c t i", i=LINE),
                 ACT.Sqrt,
             )
+
+        def distances(b, a, c0, width):
+            squares(b, a, c0, width)
+            roots(b, a, c0, width)
 
         def quantize_z(b, a, c0, width):
             cols = slice(c0, c0 + width)
@@ -223,87 +219,93 @@ def tile_list_handle_patch_deform_kernel(
                 in_=z_bf[b, a][:, cols, :].rearrange("p j t -> p (j t)"),
             )
 
-        def displace(b, first, width, g0, on_vector):
-            per_bank = min(BANK // width, WD_TILES)
-            bank = psum.tile([P, per_bank, width], F32, name="prod", tag="prod")
-            for g in range(per_bank):
-                nt = g0 + g
-                step = width if (nt < WD_TILES or width == BANK) else P
+        def tiles_per_bank(width):
+            return min(BANK // width, WD_TILES)
+
+        def displace(b, first, width, tile0, on_vector):
+            count = tiles_per_bank(width)
+            bank = psum.tile([P, count, width], F32, name="prod", tag="prod")
+            for g in range(count):
+                row_tile = tile0 + g
+                step = width if (row_tile < WD_TILES or width == BANK) else P
                 for c0 in range(0, width, step):
                     cols = slice(first + c0, first + c0 + step)
                     for a in range(PASSES):
-                        if nt < WD_TILES:
-                            rows = slice(a * N + nt * P, a * N + (nt + 1) * P)
-                            lhs, lhs_s = wd_q["words"][:, rows].bitcast(FP8X4), wd_q["scales"][:, rows]
+                        if row_tile < WD_TILES:
+                            picked_rows = slice(a * N + row_tile * P, a * N + (row_tile + 1) * P)
+                            weights = wd_q["words"][:, picked_rows].bitcast(FP8X4)
+                            weight_scales = wd_q["scales"][:, picked_rows]
                         else:
-                            m = nt - WD_TILES
-                            lhs = w4_w[:, a, m * 64 : (m + 1) * 64].bitcast(U8).bitcast(FP4X4)
-                            lhs_s = w4_s[:, a, m * 32 : (m + 1) * 32].bitcast(U8)
+                            m = row_tile - WD_TILES
+                            weights = w4_w[:, a, m * P // 2 : (m + 1) * P // 2].bitcast(U8).bitcast(FP4X4)
+                            weight_scales = w4_s[:, a, m * P // 4 : (m + 1) * P // 4].bitcast(U8)
                         nc.tensor.matmul_mx(
                             out=bank[:, g, c0 : c0 + step],
-                            lhsT=lhs,
-                            lhsT_scale=lhs_s,
+                            lhsT=weights,
+                            lhsT_scale=weight_scales,
                             rhs=z_w[b, a][:, cols].bitcast(FP8X4),
                             rhs_scale=z_s[b, a][:, cols],
                             start=(a == 0),
                             stop=(a == PASSES - 1),
                         )
-            staged = ring.tile([P, per_bank, width], F32, name="staged", bufs=8)
+            staged = ring.tile([P, count, width], F32, name="staged", bufs=STAGED_BUFS)
             if on_vector:
                 nc.vector.tensor_copy(staged[:], bank[:])
             else:
                 nc.scalar.copy(staged[:], bank[:])
             j0 = b * BANK + first
             nc.sync.dma_start(
-                out=out[g0 * P : (g0 + per_bank) * P, j0 : j0 + width].rearrange("(g p) j -> p g j", p=P),
+                out=out[tile0 * P : (tile0 + count) * P, j0 : j0 + width].rearrange("(g p) j -> p g j", p=P),
                 in_=staged[:],
             )
 
-        def whole_step(b, a):
-            squares(b, a, 0, BANK)
-            roots(b, a, 0, BANK)
+        qb_last = keep.tile([P, BANK], F32, name="qb_last")
+        nc.scalar.copy(qb_last[:].rearrange("p (n c) -> p n c", c=PACK), qb_bank[LAST][:].rearrange("p c n -> p n c"))
 
         make_base(0, 0)
         make_base(0, 1)
         gather_handles(0)
         gather_vertex_scales(0)
-        gather_vertex_words(0)
-        whole_step(0, 0)
+        gather_vertex_words(0, "vert_w")
+        distances(0, 0, 0, BANK)
         gather_handles(1)
-        whole_step(0, 1)
+        distances(0, 1, 0, BANK)
         gather_vertex_scales(1)
-        gather_vertex_scales(2)
         quantize_z(0, 0, 0, BANK)
-        gather_vertex_words(1)
-        quantize_wd()
+        gather_vertex_words(1, "base002")
         quantize_z(0, 1, 0, BANK)
 
         make_base(1, 0)
         make_base(1, 1)
-        nc.scalar.copy(qb_rows[:].rearrange("p (n c) -> p n c", c=PACK), qb_bank[2][:].rearrange("p c n -> p n c"))
-        whole_step(1, 0)
-        whole_step(1, 1)
+        distances(1, 0, 0, BANK)
+        quantize_wd()
+        for row_tile in (3, 4):
+            displace(0, 0, BANK, row_tile, False)
+        distances(1, 1, 0, BANK)
+        gather_vertex_scales(LAST)
         quantize_z(1, 0, 0, BANK)
-        gather_vertex_words(2)
+        gather_vertex_words(LAST, "vert_w")
         quantize_z(1, 1, 0, BANK)
-        for nt in range(ROW_TILES):
-            displace(0, 0, BANK, nt, False)
+        for row_tile in (5, 0, 1, 2):
+            displace(0, 0, BANK, row_tile, row_tile == 2)
 
-        make_base(2, 0)
-        make_base(2, 1)
-        whole_step(2, 0)
-        for nt in range(5):
-            displace(1, 0, BANK, nt, False)
-        squares(2, 1, 0, 256)
-        roots(2, 1, 0, 256)
-        squares(2, 1, 256, 256)
-        roots(2, 1, 256, 128)
-        roots(2, 1, 384, 128)
-        quantize_z(2, 0, 0, BANK)
-        for nt in range(5, ROW_TILES):
-            displace(1, 0, BANK, nt, True)
-        for first, width in LAST_UNITS:
-            quantize_z(2, 1, first, width)
-            per_bank = min(BANK // width, WD_TILES)
-            for g0 in range(0, ROW_TILES, per_bank):
-                displace(2, first, width, g0, (g0 // per_bank) % 2 == 1)
+        make_base(LAST, 0)
+        make_base(LAST, 1)
+        distances(LAST, 0, 0, HALF)
+        for row_tile in (0, 1):
+            displace(1, 0, BANK, row_tile, True)
+        distances(LAST, 1, 0, HALF)
+        distances(LAST, 0, HALF, HALF)
+        quantize_z(LAST, 0, 0, HALF)
+        quantize_z(LAST, 1, 0, HALF)
+        squares(LAST, 1, HALF, HALF)
+        for first, width in LAST_PIECES[1:]:
+            roots(LAST, 1, first, width)
+        quantize_z(LAST, 0, HALF, HALF)
+        for first, width in LAST_PIECES[1:]:
+            quantize_z(LAST, 1, first, width)
+        for row_tile in range(2, ROW_TILES):
+            displace(1, 0, BANK, row_tile, row_tile % 2 == 1)
+        for first, width in LAST_PIECES:
+            for index, tile0 in enumerate(range(0, ROW_TILES, tiles_per_bank(width))):
+                displace(LAST, first, width, tile0, index % 2 == 1)

@@ -31,6 +31,8 @@ TAB2_ROW = 4
 LAST_PIECES = [(0, HALF), (HALF, P), (HALF + P, P)]
 PSUM_BUFS = 4
 RING_BUFS = 3
+SQUARE_BUFS = 3
+ROUNDED_BUFS = 3
 Z_BUFS = 4
 STAGED_BUFS = 8
 
@@ -54,17 +56,23 @@ def tile_list_handle_patch_deform_kernel(
         tab_s = keep.tile([P, T // 4], I32, name="tab_s", align_bytes=64)
         qb_col = keep.tile([P, BLOCKS, PACK], F32, name="qb_col", tag="after_qb", align_bytes=64)
         hw_col = keep.tile([P, PASSES, PACK], F32, name="hw_col", tag="after_hw", align_bytes=64)
+        hw_m2 = keep.tile([P, PASSES, PACK], F32, name="hw_m2", tag="after_hw_m2", align_bytes=64)
         qa_col = keep.tile([P, PASSES, PACK], F32, name="qa_col", tag="after_qa", align_bytes=64)
         tab2_s = keep.tile([P, T2 // 4], I32, name="tab2_s", align_bytes=64)
         zeros = keep.tile([P, P], F32, name="zeros", tag="after_zeros", align_bytes=64)
         ident = keep.tile([P, P], F32, name="ident", tag="after_ident", align_bytes=64)
 
-        nc.vector.memset(tab_s[:], 0)
-        nc.vector.memset(zeros[:], 0.0)
-        nc.vector.memset(tab2_s[:], 0)
+        one = keep.tile([P, 1], F32, name="one")
+        root_of_one = keep.tile([P, 1], F32, name="root_of_one")
+
         nc.scalar.dma_start(out=qb_col[:], in_=qb.rearrange("(b p c) -> p b c", p=P, c=PACK))
+        nc.scalar.dma_start(out=hw_col[:], in_=hw.rearrange("(a p t) -> p a t", p=P, t=PACK))
         nc.gpsimd.dma_start(out=qa_col[:], in_=qa.rearrange("(a p t) -> p a t", p=P, t=PACK))
-        nc.gpsimd.dma_start(out=hw_col[:], in_=hw.rearrange("(a p t) -> p a t", p=P, t=PACK))
+        nc.gpsimd.memset(one[:], 1.0)
+        nc.scalar.activation(root_of_one[:], one[:], ACT.Sqrt)
+        nc.vector.memset(tab_s[:], 0)
+        nc.vector.memset(tab2_s[:], 0)
+        nc.vector.memset(zeros[:], 0.0)
         nc.gpsimd.affine_select(
             out=ident[:],
             in_=zeros[:],
@@ -78,34 +86,36 @@ def tile_list_handle_patch_deform_kernel(
         nc.sync.dma_start(list1[:], offs)
         nc.sync.dma_start(list2[:], offs2)
         load_scale_rows(nc, tab_s, tab_scales[0].bitcast(I32).rearrange("(q r) w -> r q w", r=4), 0)
-        tab_w = keep.tile([P, T], I32, name="tab_w", tag="after_zeros", align_bytes=64)
-        nc.sync.dma_start(out=tab_w[:], in_=tab_words[0].rearrange("p t i -> p (t i)").bitcast(I32))
         load_scale_rows(nc, tab2_s, tab2_scales[0].bitcast(I32).rearrange("(q r) w -> r q w", r=4), TAB2_ROW)
+        tab2_w = keep.tile([P, T2], I32, name="tab2_w", tag="after_zeros", align_bytes=64)
+        nc.sync.dma_start(out=tab2_w[:], in_=tab2_words[0].rearrange("p t i -> p (t i)").bitcast(I32))
 
         hw2 = keep.tile([P, PASSES, PACK], F32, name="hw2")
         hw2_qa = keep.tile([P, PASSES, PACK], F32, name="hw2_qa")
         hw2_m2 = keep.tile([P, PASSES, PACK], F32, name="hw2_m2")
         nc.gpsimd.tensor_tensor(hw2[:], hw_col[:], hw_col[:], ALU.mult)
-        nc.gpsimd.tensor_tensor(hw2_qa[:], hw2[:], qa_col[:], ALU.mult)
-        hw_m2 = keep.tile([P, PASSES, PACK], F32, name="hw_m2", tag="after_hw_m2", align_bytes=64)
         nc.gpsimd.tensor_scalar(hw_m2[:], hw_col[:], -2.0, 0.0, ALU.mult, ALU.add)
         nc.gpsimd.tensor_tensor(hw2_m2[:], hw_m2[:], hw_col[:], ALU.mult)
-        tab2_w = keep.tile([P, T2], I32, name="tab2_w", tag="after_qa", align_bytes=64)
-        nc.sync.dma_start(out=tab2_w[:], in_=tab2_words[0].rearrange("p t i -> p (t i)").bitcast(I32))
+        nc.gpsimd.tensor_tensor(hw2_qa[:], hw2[:], qa_col[:], ALU.mult)
 
-        qb_bank = []
-        for b in range(BLOCKS):
-            spread = psum.tile([P, PACK, P], F32, name=f"qb_bank{b}", tag="prod")
-            for c in range(PACK):
-                nc.tensor.transpose(spread[:, c, :], qb_col[:, b, c : c + 1].to_broadcast([P, P]), ident[:])
-            qb_bank.append(spread)
-
-        wd_raw = []
-        for a, slot in enumerate(("after_hw", "after_hw_m2")):
+        def load_wd(a, slot):
             raw = keep.tile([P, PACK, N], F32, name=f"wd_raw{a}", tag=slot, align_bytes=64)
             rows = wd[a * P * PACK : (a + 1) * P * PACK, :]
             nc.sync.dma_start(out=raw[:], in_=rows.rearrange("(p t) n -> p t n", t=PACK))
-            wd_raw.append(raw)
+            return raw
+
+        wd_raw = [load_wd(0, "after_hw_m2")]
+        tab_w = keep.tile([P, T], I32, name="tab_w", tag="after_hw", align_bytes=64)
+        nc.sync.dma_start(out=tab_w[:], in_=tab_words[0].rearrange("p t i -> p (t i)").bitcast(I32))
+        wd_raw.append(load_wd(1, "after_qa"))
+
+        qb_bank = {}
+        for b in (LAST, 0, 1):
+            spread = psum.tile([P, PACK, P], F32, name=f"qb_bank{b}", tag="prod")
+            for c in range(PACK):
+                nc.tensor.transpose(spread[:, c, :], qb_col[:, b, c : c + 1].to_broadcast([P, P]), ident[:])
+            qb_bank[b] = spread
+
         w4_w = keep.tile([P, PASSES, M // 2], I32, name="w4_w", tag="after_qb", align_bytes=64)
         nc.sync.dma_start(out=w4_w[:], in_=w4_words.bitcast(I32).rearrange("a p w -> p a w"))
         w4_s = keep.tile([P, PASSES, M // 4], I32, name="w4_s", tag="after_ident", align_bytes=64)
@@ -113,14 +123,18 @@ def tile_list_handle_patch_deform_kernel(
         load_scale_rows(nc, w4_s, w4_scales.bitcast(I32).rearrange("a (q r) w -> r q a w", r=4), 0)
 
         base, hand_w, hand_s, vert_w, vert_s, wd_q = {}, {}, {}, {}, {}, {}
-        square, z_bf, z_w, z_s = {}, {}, {}, {}
+        square, z_bf, z_w, z_s, qb_row, prod = {}, {}, {}, {}, {}, {}
+
+        def copy_qb_row(b):
+            qb_row[b] = keep.tile([P, BANK], F32, name=f"qb_row{b}")
+            nc.scalar.copy(qb_row[b][:].rearrange("p (n c) -> p n c", c=PACK), qb_bank[b][:].rearrange("p c n -> p n c"))
 
         def make_base(b, a):
             for t in range(PACK):
                 tile = keep.tile([P, BANK], F32, name=f"base{b}{a}{t}", tag=f"base{b}{a}{t}", align_bytes=64)
                 if b == LAST:
                     nc.gpsimd.tensor_scalar(
-                        tile[:], qb_last[:], hw2[:, a, t : t + 1], hw2_qa[:, a, t : t + 1], ALU.mult, ALU.add
+                        tile[:], qb_row[b][:], hw2[:, a, t : t + 1], hw2_qa[:, a, t : t + 1], ALU.mult, ALU.add
                     )
                 else:
                     nc.scalar.activation(
@@ -132,17 +146,20 @@ def tile_list_handle_patch_deform_kernel(
                     )
                 base[b, a, t] = tile
 
-        def gather_handles(a):
+        def gather_handle_scales(a):
             entries = list1[:, a * LIST_COLS : (a + 1) * LIST_COLS]
             picked = keep.tile([P, P, PACK], U8, name=f"picked{a}", align_bytes=64)
             nc.vector.tensor_copy(picked[:].rearrange("p m t -> p (m t)"), tab_s[:].bitcast(U8).indirect(entries))
             hand_s[a] = keep.tile([P, PACK, P], U8, name=f"hand_s{a}", align_bytes=64)
             nc.vector.tensor_copy(hand_s[a][:], picked[:].rearrange("p m t -> p t m"))
-            hand_w[a] = keep.tile([P, PACK, P], U32, name=f"hand_w{a}", align_bytes=64)
+
+        def gather_handle_words(a, slot):
+            entries = list1[:, a * LIST_COLS : (a + 1) * LIST_COLS]
+            hand_w[a] = keep.tile([P, PACK, P], U32, name=f"hand_w{a}", tag=slot, align_bytes=64)
             nc.vector.tensor_copy(hand_w[a][:].rearrange("p t m -> p m t"), tab_w[:].bitcast(U32).indirect(entries))
 
-        def gather_vertex_scales(b):
-            vert_s[b] = keep.tile([P, BANK], U8, name=f"vert_s{b}", align_bytes=64)
+        def gather_vertex_scales(b, slot):
+            vert_s[b] = keep.tile([P, BANK], U8, name=f"vert_s{b}", tag=slot, align_bytes=64)
             entries = list2[:, b * LIST_COLS : (b + 1) * LIST_COLS]
             nc.vector.tensor_copy(vert_s[b][:], tab2_s[:].bitcast(U8).indirect(entries))
 
@@ -151,15 +168,20 @@ def tile_list_handle_patch_deform_kernel(
             entries = list2[:, b * LIST_COLS : (b + 1) * LIST_COLS]
             nc.vector.tensor_copy(vert_w[b][:], tab2_w[:].bitcast(U32).indirect(entries))
 
-        def quantize_wd():
-            wd_bf = keep.tile([P, PASSES, N, PACK], BF16, name="wd_bf", align_bytes=64)
-            for a in range(PASSES):
-                for n0 in range(0, N, N // 2):
-                    nc.scalar.copy(
-                        wd_bf[:, a, n0 : n0 + N // 2, :].rearrange("p (c i) t -> p c t i", i=LINE),
-                        wd_raw[a][:, :, n0 : n0 + N // 2].rearrange("p t (c i) -> p c t i", i=LINE),
-                    )
-            wd_q["words"] = keep.tile([P, PASSES * N], U32, name="wd_w", tag="base003", align_bytes=64)
+        def round_wd(a, on_gpsimd):
+            if a == 0:
+                wd_q["bf"] = keep.tile([P, PASSES, N, PACK], BF16, name="wd_bf", align_bytes=64)
+            for n0 in range(0, N, N // 2):
+                rounded = wd_q["bf"][:, a, n0 : n0 + N // 2, :].rearrange("p (c i) t -> p c t i", i=LINE)
+                raw = wd_raw[a][:, :, n0 : n0 + N // 2].rearrange("p t (c i) -> p c t i", i=LINE)
+                if on_gpsimd:
+                    nc.gpsimd.tensor_scalar(rounded, raw, 1.0, 0.0, ALU.mult, ALU.add)
+                else:
+                    nc.scalar.copy(rounded, raw)
+
+        def quantize_wd(slot):
+            wd_bf = wd_q["bf"]
+            wd_q["words"] = keep.tile([P, PASSES * N], U32, name="wd_w", tag=slot, align_bytes=64)
             wd_q["scales"] = keep.tile([P, PASSES * N], U8, name="wd_s", align_bytes=64)
             flat = wd_bf[:].rearrange("p a n t -> p (a n t)")
             for c0, c1 in ((0, HALF), (HALF, PASSES * N)):
@@ -170,11 +192,7 @@ def tile_list_handle_patch_deform_kernel(
                 )
 
         def squares(b, a, c0, width):
-            if c0 == 0:
-                square[b, a] = ring.tile([P, PACK, BANK], F32, name="square")
-                z_bf[b, a] = ring.tile([P, BANK, PACK], BF16, name="z_bf", align_bytes=64)
-                z_w[b, a] = ring.tile([P, BANK], U32, name="z_w", align_bytes=64, bufs=Z_BUFS)
-                z_s[b, a] = ring.tile([P, BANK], U8, name="z_s", align_bytes=64, bufs=Z_BUFS)
+            square[b, a, c0] = ring.tile([P, PACK, width], F32, name="square", bufs=SQUARE_BUFS)
             per_bank = BANK // width
             cols = slice(c0, c0 + width)
             for t0 in range(0, PACK, per_bank):
@@ -192,7 +210,7 @@ def tile_list_handle_patch_deform_kernel(
                 for g in range(per_bank):
                     t = t0 + g
                     nc.vector.scalar_tensor_tensor(
-                        square[b, a][:, t, cols],
+                        square[b, a, c0][:, t, :],
                         dots[:, g, :],
                         hw2_m2[:, a, t : t + 1],
                         base[b, a, t][:, cols],
@@ -201,111 +219,140 @@ def tile_list_handle_patch_deform_kernel(
                     )
 
         def roots(b, a, c0, width):
+            z_bf[b, a, c0] = ring.tile([P, width, PACK], BF16, name="z_bf", align_bytes=64, bufs=ROUNDED_BUFS)
             nc.scalar.activation(
-                z_bf[b, a][:, c0 : c0 + width, :].rearrange("p (c i) t -> p c t i", i=LINE),
-                square[b, a][:, :, c0 : c0 + width].rearrange("p t (c i) -> p c t i", i=LINE),
+                z_bf[b, a, c0][:].rearrange("p (c i) t -> p c t i", i=LINE),
+                square[b, a, c0][:].rearrange("p t (c i) -> p c t i", i=LINE),
                 ACT.Sqrt,
             )
 
-        def distances(b, a, c0, width):
-            squares(b, a, c0, width)
-            roots(b, a, c0, width)
-
         def quantize_z(b, a, c0, width):
+            if c0 == 0:
+                z_w[b, a] = ring.tile([P, BANK], U32, name="z_w", align_bytes=64, bufs=Z_BUFS)
+                z_s[b, a] = ring.tile([P, BANK], U8, name="z_s", align_bytes=64, bufs=Z_BUFS)
             cols = slice(c0, c0 + width)
             nc.vector.quantize_mx(
                 out=z_w[b, a][:, cols].bitcast(FP8X4),
                 scales=z_s[b, a][:, cols],
-                in_=z_bf[b, a][:, cols, :].rearrange("p j t -> p (j t)"),
+                in_=z_bf[b, a, c0][:].rearrange("p j t -> p (j t)"),
             )
 
         def tiles_per_bank(width):
             return min(BANK // width, WD_TILES)
 
-        def displace(b, first, width, tile0, on_vector):
+        def multiply(b, a, first, width, tile0, tag="prod"):
             count = tiles_per_bank(width)
-            bank = psum.tile([P, count, width], F32, name="prod", tag="prod")
+            if a == 0:
+                prod[b, first, tile0] = psum.tile([P, count, width], F32, name="prod", tag=tag)
+            bank = prod[b, first, tile0]
             for g in range(count):
                 row_tile = tile0 + g
                 step = width if (row_tile < WD_TILES or width == BANK) else P
                 for c0 in range(0, width, step):
                     cols = slice(first + c0, first + c0 + step)
-                    for a in range(PASSES):
-                        if row_tile < WD_TILES:
-                            picked_rows = slice(a * N + row_tile * P, a * N + (row_tile + 1) * P)
-                            weights = wd_q["words"][:, picked_rows].bitcast(FP8X4)
-                            weight_scales = wd_q["scales"][:, picked_rows]
-                        else:
-                            m = row_tile - WD_TILES
-                            weights = w4_w[:, a, m * P // 2 : (m + 1) * P // 2].bitcast(U8).bitcast(FP4X4)
-                            weight_scales = w4_s[:, a, m * P // 4 : (m + 1) * P // 4].bitcast(U8)
-                        nc.tensor.matmul_mx(
-                            out=bank[:, g, c0 : c0 + step],
-                            lhsT=weights,
-                            lhsT_scale=weight_scales,
-                            rhs=z_w[b, a][:, cols].bitcast(FP8X4),
-                            rhs_scale=z_s[b, a][:, cols],
-                            start=(a == 0),
-                            stop=(a == PASSES - 1),
-                        )
+                    if row_tile < WD_TILES:
+                        picked_rows = slice(a * N + row_tile * P, a * N + (row_tile + 1) * P)
+                        weights = wd_q["words"][:, picked_rows].bitcast(FP8X4)
+                        weight_scales = wd_q["scales"][:, picked_rows]
+                    else:
+                        m = row_tile - WD_TILES
+                        weights = w4_w[:, a, m * P // 2 : (m + 1) * P // 2].bitcast(U8).bitcast(FP4X4)
+                        weight_scales = w4_s[:, a, m * P // 4 : (m + 1) * P // 4].bitcast(U8)
+                    nc.tensor.matmul_mx(
+                        out=bank[:, g, c0 : c0 + step],
+                        lhsT=weights,
+                        lhsT_scale=weight_scales,
+                        rhs=z_w[b, a][:, cols].bitcast(FP8X4),
+                        rhs_scale=z_s[b, a][:, cols],
+                        start=(a == 0 and g == 0 and c0 == 0),
+                        stop=(a == PASSES - 1 and g == count - 1 and c0 + step == width),
+                    )
+
+        def store(b, first, width, tile0, on_vector):
+            count = tiles_per_bank(width)
             staged = ring.tile([P, count, width], F32, name="staged", bufs=STAGED_BUFS)
             if on_vector:
-                nc.vector.tensor_copy(staged[:], bank[:])
+                nc.vector.tensor_copy(staged[:], prod[b, first, tile0][:])
             else:
-                nc.scalar.copy(staged[:], bank[:])
+                nc.scalar.copy(staged[:], prod[b, first, tile0][:])
             j0 = b * BANK + first
             nc.sync.dma_start(
                 out=out[tile0 * P : (tile0 + count) * P, j0 : j0 + width].rearrange("(g p) j -> p g j", p=P),
                 in_=staged[:],
             )
 
-        qb_last = keep.tile([P, BANK], F32, name="qb_last")
-        nc.scalar.copy(qb_last[:].rearrange("p (n c) -> p n c", c=PACK), qb_bank[LAST][:].rearrange("p c n -> p n c"))
+        def displace(b, first, width, tile0, on_vector):
+            for a in range(PASSES):
+                multiply(b, a, first, width, tile0)
+            store(b, first, width, tile0, on_vector)
 
-        make_base(0, 0)
-        make_base(0, 1)
-        gather_handles(0)
-        gather_vertex_scales(0)
-        gather_vertex_words(0, "vert_w")
-        distances(0, 0, 0, BANK)
-        gather_handles(1)
-        distances(0, 1, 0, BANK)
-        gather_vertex_scales(1)
-        quantize_z(0, 0, 0, BANK)
-        gather_vertex_words(1, "base002")
-        quantize_z(0, 1, 0, BANK)
-
-        make_base(1, 0)
-        make_base(1, 1)
-        distances(1, 0, 0, BANK)
-        quantize_wd()
-        for row_tile in (3, 4):
-            displace(0, 0, BANK, row_tile, False)
-        distances(1, 1, 0, BANK)
-        gather_vertex_scales(LAST)
-        quantize_z(1, 0, 0, BANK)
-        gather_vertex_words(LAST, "vert_w")
-        quantize_z(1, 1, 0, BANK)
-        for row_tile in (5, 0, 1, 2):
-            displace(0, 0, BANK, row_tile, row_tile == 2)
-
+        copy_qb_row(LAST)
         make_base(LAST, 0)
         make_base(LAST, 1)
-        distances(LAST, 0, 0, HALF)
-        for row_tile in (0, 1):
-            displace(1, 0, BANK, row_tile, True)
-        distances(LAST, 1, 0, HALF)
-        distances(LAST, 0, HALF, HALF)
-        quantize_z(LAST, 0, 0, HALF)
-        quantize_z(LAST, 1, 0, HALF)
-        squares(LAST, 1, HALF, HALF)
-        for first, width in LAST_PIECES[1:]:
-            roots(LAST, 1, first, width)
-        quantize_z(LAST, 0, HALF, HALF)
-        for first, width in LAST_PIECES[1:]:
-            quantize_z(LAST, 1, first, width)
-        for row_tile in range(2, ROW_TILES):
-            displace(1, 0, BANK, row_tile, row_tile % 2 == 1)
-        for first, width in LAST_PIECES:
-            for index, tile0 in enumerate(range(0, ROW_TILES, tiles_per_bank(width))):
-                displace(LAST, first, width, tile0, index % 2 == 1)
+        make_base(0, 0)
+        make_base(0, 1)
+        make_base(1, 0)
+        round_wd(0, False)
+        make_base(1, 1)
+        round_wd(1, False)
+        gather_handle_scales(0)
+        gather_handle_scales(1)
+        gather_vertex_scales(0, "vert_s0")
+        gather_vertex_scales(1, "vert_s1")
+        gather_vertex_scales(2, "vert_s2")
+        gather_vertex_words(0, "vert_w0")
+        gather_vertex_words(1, "vert_w1")
+        gather_vertex_words(2, "vert_w2")
+        gather_handle_words(0, "hand_w0")
+        gather_handle_words(1, "hand_w1")
+        squares(0, 0, 0, BANK)
+        roots(0, 0, 0, BANK)
+        squares(0, 1, 0, BANK)
+        roots(0, 1, 0, BANK)
+        quantize_z(0, 0, 0, BANK)
+        squares(1, 0, 0, BANK)
+        quantize_z(0, 1, 0, BANK)
+        quantize_wd("wd_w")
+        squares(1, 1, 0, BANK)
+        roots(1, 0, 0, BANK)
+        displace(0, 0, BANK, 3, False)
+        displace(0, 0, BANK, 4, False)
+        displace(0, 0, BANK, 5, True)
+        displace(0, 0, BANK, 0, False)
+        roots(1, 1, 0, BANK)
+        displace(0, 0, BANK, 1, False)
+        displace(0, 0, BANK, 2, True)
+        quantize_z(1, 0, 0, BANK)
+        squares(2, 0, 0, HALF)
+        quantize_z(1, 1, 0, BANK)
+        squares(2, 1, 0, HALF)
+        displace(1, 0, BANK, 0, False)
+        roots(2, 0, 0, HALF)
+        displace(1, 0, BANK, 1, True)
+        squares(2, 0, HALF, HALF)
+        displace(1, 0, BANK, 2, False)
+        roots(2, 1, 0, HALF)
+        quantize_z(2, 0, 0, HALF)
+        squares(2, 1, HALF, P)
+        displace(1, 0, BANK, 3, False)
+        quantize_z(2, 1, 0, HALF)
+        squares(2, 1, HALF + P, P)
+        roots(2, 0, HALF, HALF)
+        displace(1, 0, BANK, 4, True)
+        displace(1, 0, BANK, 5, False)
+        roots(2, 1, HALF, P)
+        quantize_z(2, 0, HALF, HALF)
+        roots(2, 1, HALF + P, P)
+        displace(2, 0, HALF, 0, True)
+        quantize_z(2, 1, HALF, P)
+        displace(2, 0, HALF, 2, False)
+        displace(2, 0, HALF, 4, True)
+        multiply(2, 0, HALF + P, P, 0, "dots")
+        multiply(2, 0, HALF + P, P, 3, "dots")
+        quantize_z(2, 1, HALF + P, P)
+        displace(2, HALF, P, 0, False)
+        displace(2, HALF, P, 3, True)
+        multiply(2, 1, HALF + P, P, 0)
+        store(2, HALF + P, P, 0, False)
+        multiply(2, 1, HALF + P, P, 3)
+        store(2, HALF + P, P, 3, True)

@@ -37,9 +37,9 @@ Z_BUFS = 4
 STAGED_BUFS = 8
 
 
-def load_scale_rows(nc, tile, rows, first):
+def load_scale_rows(queue, tile, rows, first):
     for r in range(4):
-        nc.sync.dma_start(out=tile[first + r : P : 32], in_=rows[r])
+        queue.dma_start(out=tile[first + r : P : 32], in_=rows[r])
 
 
 def tile_list_handle_patch_deform_kernel(
@@ -49,30 +49,29 @@ def tile_list_handle_patch_deform_kernel(
     with ExitStack() as ctx:
         keep = ctx.enter_context(tc.tile_pool(name="keep", bufs=1))
         ring = ctx.enter_context(tc.tile_pool(name="ring", bufs=RING_BUFS))
+        shared = ctx.enter_context(tc.tile_pool(name="shared", bufs=1))
         psum = ctx.enter_context(tc.psum_pool(name="psum", bufs=PSUM_BUFS))
 
         list1 = keep.tile([P, S // 16], U16, name="list1")
         list2 = keep.tile([P, S2 // 16], U16, name="list2")
         tab_s = keep.tile([P, T // 4], I32, name="tab_s", align_bytes=64)
-        qb_col = keep.tile([P, BLOCKS, PACK], F32, name="qb_col", tag="after_qb", align_bytes=64)
-        hw_col = keep.tile([P, PASSES, PACK], F32, name="hw_col", tag="after_hw", align_bytes=64)
-        hw_m2 = keep.tile([P, PASSES, PACK], F32, name="hw_m2", tag="after_hw_m2", align_bytes=64)
-        qa_col = keep.tile([P, PASSES, PACK], F32, name="qa_col", tag="after_qa", align_bytes=64)
         tab2_s = keep.tile([P, T2 // 4], I32, name="tab2_s", align_bytes=64)
+        qb_col = shared.tile([P, BLOCKS, PACK], F32, name="qb_col", offset=2048, align_bytes=64)
+        hw_col = keep.tile([P, PASSES, PACK], F32, name="hw_col", tag="after_hw", align_bytes=64)
+        qa_col = keep.tile([P, PASSES, PACK], F32, name="qa_col", tag="after_qa", align_bytes=64)
         zeros = keep.tile([P, P], F32, name="zeros", tag="after_zeros", align_bytes=64)
         ident = keep.tile([P, P], F32, name="ident", tag="after_ident", align_bytes=64)
-
         one = keep.tile([P, 1], F32, name="one")
         root_of_one = keep.tile([P, 1], F32, name="root_of_one")
 
-        nc.scalar.dma_start(out=qb_col[:], in_=qb.rearrange("(b p c) -> p b c", p=P, c=PACK))
+        nc.gpsimd.dma_start(out=qb_col[:], in_=qb.rearrange("(b p c) -> p b c", p=P, c=PACK))
         nc.scalar.dma_start(out=hw_col[:], in_=hw.rearrange("(a p t) -> p a t", p=P, t=PACK))
-        nc.gpsimd.dma_start(out=qa_col[:], in_=qa.rearrange("(a p t) -> p a t", p=P, t=PACK))
-        nc.gpsimd.memset(one[:], 1.0)
-        nc.scalar.activation(root_of_one[:], one[:], ACT.Sqrt)
+        nc.scalar.dma_start(out=qa_col[:], in_=qa.rearrange("(a p t) -> p a t", p=P, t=PACK))
         nc.vector.memset(tab_s[:], 0)
-        nc.vector.memset(tab2_s[:], 0)
+        nc.vector.memset(one[:], 1.0)
+        nc.scalar.activation(root_of_one[:], one[:], ACT.Sqrt)
         nc.vector.memset(zeros[:], 0.0)
+        nc.vector.memset(tab2_s[:], 0)
         nc.gpsimd.affine_select(
             out=ident[:],
             in_=zeros[:],
@@ -85,54 +84,49 @@ def tile_list_handle_patch_deform_kernel(
 
         nc.sync.dma_start(list1[:], offs)
         nc.sync.dma_start(list2[:], offs2)
-        load_scale_rows(nc, tab_s, tab_scales[0].bitcast(I32).rearrange("(q r) w -> r q w", r=4), 0)
-        load_scale_rows(nc, tab2_s, tab2_scales[0].bitcast(I32).rearrange("(q r) w -> r q w", r=4), TAB2_ROW)
-        tab2_w = keep.tile([P, T2], I32, name="tab2_w", tag="after_zeros", align_bytes=64)
-        nc.sync.dma_start(out=tab2_w[:], in_=tab2_words[0].rearrange("p t i -> p (t i)").bitcast(I32))
+        load_scale_rows(nc.sync, tab_s, tab_scales[0].bitcast(I32).rearrange("(q r) w -> r q w", r=4), 0)
+        tab_w = keep.tile([P, T], I32, name="tab_w", tag="after_zeros", align_bytes=64)
+        nc.sync.dma_start(out=tab_w[:], in_=tab_words[0].rearrange("p t i -> p (t i)").bitcast(I32))
+        load_scale_rows(nc.sync, tab2_s, tab2_scales[0].bitcast(I32).rearrange("(q r) w -> r q w", r=4), TAB2_ROW)
 
         hw2 = keep.tile([P, PASSES, PACK], F32, name="hw2")
         hw2_qa = keep.tile([P, PASSES, PACK], F32, name="hw2_qa")
         hw2_m2 = keep.tile([P, PASSES, PACK], F32, name="hw2_m2")
-        nc.gpsimd.tensor_tensor(hw2[:], hw_col[:], hw_col[:], ALU.mult)
-        nc.gpsimd.tensor_scalar(hw_m2[:], hw_col[:], -2.0, 0.0, ALU.mult, ALU.add)
-        nc.gpsimd.tensor_tensor(hw2_m2[:], hw_m2[:], hw_col[:], ALU.mult)
-        nc.gpsimd.tensor_tensor(hw2_qa[:], hw2[:], qa_col[:], ALU.mult)
-
-        def load_wd(a, slot):
-            raw = keep.tile([P, PACK, N], F32, name=f"wd_raw{a}", tag=slot, align_bytes=64)
-            rows = wd[a * P * PACK : (a + 1) * P * PACK, :]
-            nc.sync.dma_start(out=raw[:], in_=rows.rearrange("(p t) n -> p t n", t=PACK))
-            return raw
-
-        wd_raw = [load_wd(0, "after_hw_m2")]
-        tab_w = keep.tile([P, T], I32, name="tab_w", tag="after_hw", align_bytes=64)
-        nc.sync.dma_start(out=tab_w[:], in_=tab_words[0].rearrange("p t i -> p (t i)").bitcast(I32))
-        wd_raw.append(load_wd(1, "after_qa"))
+        nc.vector.tensor_tensor(hw2[:], hw_col[:], hw_col[:], ALU.mult)
+        nc.vector.scalar_tensor_tensor(hw2_m2[:], hw_col[:], -2.0, hw_col[:], ALU.mult, ALU.mult)
+        nc.vector.tensor_tensor(hw2_qa[:], hw2[:], qa_col[:], ALU.mult)
+        tab2_w = keep.tile([P, T2], I32, name="tab2_w", tag="after_hw", align_bytes=64)
+        nc.sync.dma_start(out=tab2_w[:], in_=tab2_words[0].rearrange("p t i -> p (t i)").bitcast(I32))
 
         qb_bank = {}
-        for b in (LAST, 0, 1):
+        for b in (0, LAST, 1):
             spread = psum.tile([P, PACK, P], F32, name=f"qb_bank{b}", tag="prod")
             for c in range(PACK):
                 nc.tensor.transpose(spread[:, c, :], qb_col[:, b, c : c + 1].to_broadcast([P, P]), ident[:])
             qb_bank[b] = spread
 
-        w4_w = keep.tile([P, PASSES, M // 2], I32, name="w4_w", tag="after_qb", align_bytes=64)
-        nc.sync.dma_start(out=w4_w[:], in_=w4_words.bitcast(I32).rearrange("a p w -> p a w"))
+        wd_raw = [
+            keep.tile([P, PACK, N], F32, name="wd_raw0", tag="after_qa", align_bytes=64),
+            shared.tile([P, PACK, N], F32, name="wd_raw1", offset=2048, align_bytes=64),
+        ]
+        for a in range(PASSES):
+            rows = wd[a * P * PACK : (a + 1) * P * PACK, :]
+            nc.sync.dma_start(out=wd_raw[a][:], in_=rows.rearrange("(p t) n -> p t n", t=PACK))
         w4_s = keep.tile([P, PASSES, M // 4], I32, name="w4_s", tag="after_ident", align_bytes=64)
         nc.gpsimd.memset(w4_s[:], 0)
-        load_scale_rows(nc, w4_s, w4_scales.bitcast(I32).rearrange("a (q r) w -> r q a w", r=4), 0)
+        load_scale_rows(nc.sync, w4_s, w4_scales.bitcast(I32).rearrange("a (q r) w -> r q a w", r=4), 0)
 
         base, hand_w, hand_s, vert_w, vert_s, wd_q = {}, {}, {}, {}, {}, {}
         square, z_bf, z_w, z_s, qb_row, prod = {}, {}, {}, {}, {}, {}
 
         def copy_qb_row(b):
-            qb_row[b] = keep.tile([P, BANK], F32, name=f"qb_row{b}")
+            qb_row[b] = keep.tile([P, BANK], F32, name=f"qb_row{b}", align_bytes=64)
             nc.scalar.copy(qb_row[b][:].rearrange("p (n c) -> p n c", c=PACK), qb_bank[b][:].rearrange("p c n -> p n c"))
 
         def make_base(b, a):
             for t in range(PACK):
                 tile = keep.tile([P, BANK], F32, name=f"base{b}{a}{t}", tag=f"base{b}{a}{t}", align_bytes=64)
-                if b == LAST:
+                if (b, a) >= (LAST, 0):
                     nc.gpsimd.tensor_scalar(
                         tile[:], qb_row[b][:], hw2[:, a, t : t + 1], hw2_qa[:, a, t : t + 1], ALU.mult, ALU.add
                     )
@@ -179,9 +173,9 @@ def tile_list_handle_patch_deform_kernel(
                 else:
                     nc.scalar.copy(rounded, raw)
 
-        def quantize_wd(slot):
+        def quantize_wd(at):
             wd_bf = wd_q["bf"]
-            wd_q["words"] = keep.tile([P, PASSES * N], U32, name="wd_w", tag=slot, align_bytes=64)
+            wd_q["words"] = shared.tile([P, PASSES * N], U32, name="wd_w", offset=at, align_bytes=64)
             wd_q["scales"] = keep.tile([P, PASSES * N], U8, name="wd_s", align_bytes=64)
             flat = wd_bf[:].rearrange("p a n t -> p (a n t)")
             for c0, c1 in ((0, HALF), (HALF, PASSES * N)):
@@ -191,8 +185,11 @@ def tile_list_handle_patch_deform_kernel(
                     in_=flat[:, PACK * c0 : PACK * c1],
                 )
 
-        def squares(b, a, c0, width):
-            square[b, a, c0] = ring.tile([P, PACK, width], F32, name="square", bufs=SQUARE_BUFS)
+        def squares(b, a, c0, width, at=None):
+            if at is None:
+                square[b, a, c0] = ring.tile([P, PACK, width], F32, name="square", bufs=SQUARE_BUFS)
+            else:
+                square[b, a, c0] = shared.tile([P, PACK, width], F32, name=f"square{b}{a}{c0}", offset=at, align_bytes=64)
             per_bank = BANK // width
             cols = slice(c0, c0 + width)
             for t0 in range(0, PACK, per_bank):
@@ -218,11 +215,15 @@ def tile_list_handle_patch_deform_kernel(
                         ALU.add,
                     )
 
-        def roots(b, a, c0, width):
-            z_bf[b, a, c0] = ring.tile([P, width, PACK], BF16, name="z_bf", align_bytes=64, bufs=ROUNDED_BUFS)
+        def roots(b, a, c0, width, at=None):
+            if at is None:
+                z_bf[b, a, c0] = ring.tile([P, width, PACK], BF16, name="z_bf", align_bytes=64, bufs=ROUNDED_BUFS)
+            else:
+                z_bf[b, a, c0] = shared.tile([P, width, PACK], BF16, name=f"z_bf{b}{a}{c0}", offset=at, align_bytes=64)
+            s0 = max(c for (bb, aa, c) in square if (bb, aa) == (b, a) and c <= c0)
             nc.scalar.activation(
                 z_bf[b, a, c0][:].rearrange("p (c i) t -> p c t i", i=LINE),
-                square[b, a, c0][:].rearrange("p t (c i) -> p c t i", i=LINE),
+                square[b, a, s0][:, :, c0 - s0 : c0 - s0 + width].rearrange("p t (c i) -> p c t i", i=LINE),
                 ACT.Sqrt,
             )
 
@@ -240,15 +241,16 @@ def tile_list_handle_patch_deform_kernel(
         def tiles_per_bank(width):
             return min(BANK // width, WD_TILES)
 
-        def multiply(b, a, first, width, tile0, tag="prod"):
+        def multiply(b, a, first, width, tile0, tag="prod", part=None):
             count = tiles_per_bank(width)
             if a == 0:
                 prod[b, first, tile0] = psum.tile([P, count, width], F32, name="prod", tag=tag)
             bank = prod[b, first, tile0]
             for g in range(count):
                 row_tile = tile0 + g
-                step = width if (row_tile < WD_TILES or width == BANK) else P
-                for c0 in range(0, width, step):
+                lo, hi = (0, width) if part is None else part
+                step = hi - lo if (row_tile < WD_TILES or width == BANK) else P
+                for c0 in range(lo, hi, step):
                     cols = slice(first + c0, first + c0 + step)
                     if row_tile < WD_TILES:
                         picked_rows = slice(a * N + row_tile * P, a * N + (row_tile + 1) * P)
@@ -289,43 +291,47 @@ def tile_list_handle_patch_deform_kernel(
         copy_qb_row(LAST)
         make_base(LAST, 0)
         make_base(LAST, 1)
+        w4_w = keep.tile([P, PASSES, M // 2], I32, name="w4_w", tag="qb_row2", align_bytes=64)
+        nc.sync.dma_start(out=w4_w[:], in_=w4_words.bitcast(I32).rearrange("a p w -> p a w"))
         make_base(0, 0)
         make_base(0, 1)
         make_base(1, 0)
-        round_wd(0, False)
         make_base(1, 1)
+        round_wd(0, False)
         round_wd(1, False)
         gather_handle_scales(0)
         gather_handle_scales(1)
-        gather_vertex_scales(0, "vert_s0")
-        gather_vertex_scales(1, "vert_s1")
-        gather_vertex_scales(2, "vert_s2")
-        gather_vertex_words(0, "vert_w0")
-        gather_vertex_words(1, "vert_w1")
-        gather_vertex_words(2, "vert_w2")
         gather_handle_words(0, "hand_w0")
         gather_handle_words(1, "hand_w1")
+        gather_vertex_scales(0, "vert_s0")
+        gather_vertex_scales(1, "vert_s1")
+        gather_vertex_words(0, "vert_w0")
+        gather_vertex_words(1, "vert_w1")
         squares(0, 0, 0, BANK)
-        roots(0, 0, 0, BANK)
+        roots(0, 0, 0, BANK, 0)
         squares(0, 1, 0, BANK)
-        roots(0, 1, 0, BANK)
-        quantize_z(0, 0, 0, BANK)
+        roots(0, 1, 0, HALF, 6144)
+        roots(0, 1, HALF, HALF, 4096)
         squares(1, 0, 0, BANK)
-        quantize_z(0, 1, 0, BANK)
-        quantize_wd("wd_w")
-        squares(1, 1, 0, BANK)
+        quantize_z(0, 0, 0, BANK)
+        quantize_wd(0)
+        quantize_z(0, 1, 0, HALF)
+        quantize_z(0, 1, HALF, HALF)
+        squares(1, 1, 0, BANK, 7168)
         roots(1, 0, 0, BANK)
+        quantize_z(1, 0, 0, BANK)
         displace(0, 0, BANK, 3, False)
         displace(0, 0, BANK, 4, False)
-        displace(0, 0, BANK, 5, True)
+        displace(0, 0, BANK, 5, False)
+        roots(1, 1, 0, BANK, 16384)
+        gather_vertex_scales(2, "base111")
+        gather_vertex_words(2, "base112")
         displace(0, 0, BANK, 0, False)
-        roots(1, 1, 0, BANK)
         displace(0, 0, BANK, 1, False)
-        displace(0, 0, BANK, 2, True)
-        quantize_z(1, 0, 0, BANK)
-        squares(2, 0, 0, HALF)
+        displace(0, 0, BANK, 2, False)
         quantize_z(1, 1, 0, BANK)
-        squares(2, 1, 0, HALF)
+        squares(2, 0, 0, HALF, 14336)
+        squares(2, 1, 0, HALF, 18432)
         displace(1, 0, BANK, 0, False)
         roots(2, 0, 0, HALF)
         displace(1, 0, BANK, 1, True)
@@ -333,26 +339,30 @@ def tile_list_handle_patch_deform_kernel(
         displace(1, 0, BANK, 2, False)
         roots(2, 1, 0, HALF)
         quantize_z(2, 0, 0, HALF)
-        squares(2, 1, HALF, P)
-        displace(1, 0, BANK, 3, False)
+        displace(1, 0, BANK, 3, True)
         quantize_z(2, 1, 0, HALF)
+        squares(2, 1, HALF, P)
         squares(2, 1, HALF + P, P)
+        displace(1, 0, BANK, 4, False)
         roots(2, 0, HALF, HALF)
-        displace(1, 0, BANK, 4, True)
         displace(1, 0, BANK, 5, False)
-        roots(2, 1, HALF, P)
         quantize_z(2, 0, HALF, HALF)
-        roots(2, 1, HALF + P, P)
         displace(2, 0, HALF, 0, True)
+        roots(2, 1, HALF, P)
+        roots(2, 1, HALF + P, P)
         quantize_z(2, 1, HALF, P)
-        displace(2, 0, HALF, 2, False)
-        displace(2, 0, HALF, 4, True)
-        multiply(2, 0, HALF + P, P, 0, "dots")
-        multiply(2, 0, HALF + P, P, 3, "dots")
+        multiply(2, 0, HALF, HALF, 0, "dots")
+        multiply(2, 0, HALF, HALF, 2, "dots")
+        multiply(2, 0, HALF, HALF, 4, "dots")
+        displace(2, 0, HALF, 2, True)
         quantize_z(2, 1, HALF + P, P)
-        displace(2, HALF, P, 0, False)
-        displace(2, HALF, P, 3, True)
-        multiply(2, 1, HALF + P, P, 0)
-        store(2, HALF + P, P, 0, False)
-        multiply(2, 1, HALF + P, P, 3)
-        store(2, HALF + P, P, 3, True)
+        displace(2, 0, HALF, 4, False)
+        multiply(LAST, 1, HALF, HALF, 0, part=(0, P))
+        multiply(LAST, 1, HALF, HALF, 2, part=(0, P))
+        multiply(LAST, 1, HALF, HALF, 4, part=(0, P))
+        multiply(LAST, 1, HALF, HALF, 0, part=(P, HALF))
+        store(2, HALF, HALF, 0, False)
+        multiply(LAST, 1, HALF, HALF, 2, part=(P, HALF))
+        store(2, HALF, HALF, 2, True)
+        multiply(LAST, 1, HALF, HALF, 4, part=(P, HALF))
+        store(2, HALF, HALF, 4, False)

@@ -29,7 +29,7 @@ WD_TILES = N // P
 LINE = 4
 TAB2_ROW = 4
 LAST_PIECES = [(0, HALF), (HALF, P), (HALF + P, P)]
-PSUM_BUFS = 4
+PSUM_BUFS = 1
 RING_BUFS = 3
 SQUARE_BUFS = 3
 ROUNDED_BUFS = 3
@@ -56,9 +56,9 @@ def tile_list_handle_patch_deform_kernel(
         list2 = keep.tile([P, S2 // 16], U16, name="list2")
         tab_s = keep.tile([P, T // 4], I32, name="tab_s", align_bytes=64)
         tab2_s = keep.tile([P, T2 // 4], I32, name="tab2_s", align_bytes=64)
-        qb_col = shared.tile([P, BLOCKS, PACK], F32, name="qb_col", offset=2048, align_bytes=64)
+        qb_col = keep.tile([P, BLOCKS, PACK], F32, name="qb_col", tag="after_qb", align_bytes=64)
         hw_col = keep.tile([P, PASSES, PACK], F32, name="hw_col", tag="after_hw", align_bytes=64)
-        qa_col = keep.tile([P, PASSES, PACK], F32, name="qa_col", tag="after_qa", align_bytes=64)
+        qa_col = shared.tile([P, PASSES, PACK], F32, name="qa_col", offset=2048, align_bytes=64)
         zeros = keep.tile([P, P], F32, name="zeros", tag="after_zeros", align_bytes=64)
         ident = keep.tile([P, P], F32, name="ident", tag="after_ident", align_bytes=64)
         one = keep.tile([P, 1], F32, name="one")
@@ -99,15 +99,15 @@ def tile_list_handle_patch_deform_kernel(
         nc.sync.dma_start(out=tab2_w[:], in_=tab2_words[0].rearrange("p t i -> p (t i)").bitcast(I32))
 
         qb_bank = {}
-        for b in (0, LAST, 1):
-            spread = psum.tile([P, PACK, P], F32, name=f"qb_bank{b}", tag="prod")
+        for b in (1, 0, LAST):
+            spread = psum.tile([P, PACK, P], F32, name=f"qb_bank{b}", tag=f"bank{4 + b}")
             for c in range(PACK):
                 nc.tensor.transpose(spread[:, c, :], qb_col[:, b, c : c + 1].to_broadcast([P, P]), ident[:])
             qb_bank[b] = spread
 
         wd_raw = [
-            keep.tile([P, PACK, N], F32, name="wd_raw0", tag="after_qa", align_bytes=64),
-            shared.tile([P, PACK, N], F32, name="wd_raw1", offset=2048, align_bytes=64),
+            shared.tile([P, PACK, N], F32, name="wd_raw0", offset=2048, align_bytes=64),
+            keep.tile([P, PACK, N], F32, name="wd_raw1", tag="after_qb", align_bytes=64),
         ]
         for a in range(PASSES):
             rows = wd[a * P * PACK : (a + 1) * P * PACK, :]
@@ -116,7 +116,8 @@ def tile_list_handle_patch_deform_kernel(
         nc.gpsimd.memset(w4_s[:], 0)
         load_scale_rows(nc.sync, w4_s, w4_scales.bitcast(I32).rearrange("a (q r) w -> r q a w", r=4), 0)
 
-        base, hand_w, hand_s, vert_w, vert_s, wd_q = {}, {}, {}, {}, {}, {}
+        base, hand_w, hand_s, vert_w, vert_s = {}, {}, {}, {}, {}
+        wd_bf, wd_w, wd_s = {}, {}, {}
         square, z_bf, z_w, z_s, qb_row, prod = {}, {}, {}, {}, {}, {}
 
         def copy_qb_row(b):
@@ -126,7 +127,7 @@ def tile_list_handle_patch_deform_kernel(
         def make_base(b, a):
             for t in range(PACK):
                 tile = keep.tile([P, BANK], F32, name=f"base{b}{a}{t}", tag=f"base{b}{a}{t}", align_bytes=64)
-                if (b, a) >= (LAST, 0):
+                if (b, a) >= (1, 1):
                     nc.gpsimd.tensor_scalar(
                         tile[:], qb_row[b][:], hw2[:, a, t : t + 1], hw2_qa[:, a, t : t + 1], ALU.mult, ALU.add
                     )
@@ -157,43 +158,44 @@ def tile_list_handle_patch_deform_kernel(
             entries = list2[:, b * LIST_COLS : (b + 1) * LIST_COLS]
             nc.vector.tensor_copy(vert_s[b][:], tab2_s[:].bitcast(U8).indirect(entries))
 
-        def gather_vertex_words(b, slot):
-            vert_w[b] = keep.tile([P, BANK], U32, name=f"vert_w{b}", tag=slot, align_bytes=64)
+        def gather_vertex_words(b, slot, at=None):
+            if at is None:
+                vert_w[b] = keep.tile([P, BANK], U32, name=f"vert_w{b}", tag=slot, align_bytes=64)
+            else:
+                vert_w[b] = shared.tile([P, BANK], U32, name=f"vert_w{b}", offset=at, align_bytes=64)
             entries = list2[:, b * LIST_COLS : (b + 1) * LIST_COLS]
             nc.vector.tensor_copy(vert_w[b][:], tab2_w[:].bitcast(U32).indirect(entries))
 
-        def round_wd(a, on_gpsimd):
-            if a == 0:
-                wd_q["bf"] = keep.tile([P, PASSES, N, PACK], BF16, name="wd_bf", align_bytes=64)
+        def round_wd(a, at=None):
+            if at is None:
+                wd_bf[a] = keep.tile([P, N, PACK], BF16, name=f"wd_bf{a}", align_bytes=64)
+            else:
+                wd_bf[a] = shared.tile([P, N, PACK], BF16, name=f"wd_bf{a}", offset=at, align_bytes=64)
             for n0 in range(0, N, N // 2):
-                rounded = wd_q["bf"][:, a, n0 : n0 + N // 2, :].rearrange("p (c i) t -> p c t i", i=LINE)
-                raw = wd_raw[a][:, :, n0 : n0 + N // 2].rearrange("p t (c i) -> p c t i", i=LINE)
-                if on_gpsimd:
-                    nc.gpsimd.tensor_scalar(rounded, raw, 1.0, 0.0, ALU.mult, ALU.add)
-                else:
-                    nc.scalar.copy(rounded, raw)
-
-        def quantize_wd(at):
-            wd_bf = wd_q["bf"]
-            wd_q["words"] = shared.tile([P, PASSES * N], U32, name="wd_w", offset=at, align_bytes=64)
-            wd_q["scales"] = keep.tile([P, PASSES * N], U8, name="wd_s", align_bytes=64)
-            flat = wd_bf[:].rearrange("p a n t -> p (a n t)")
-            for c0, c1 in ((0, HALF), (HALF, PASSES * N)):
-                nc.vector.quantize_mx(
-                    out=wd_q["words"][:, c0:c1].bitcast(FP8X4),
-                    scales=wd_q["scales"][:, c0:c1],
-                    in_=flat[:, PACK * c0 : PACK * c1],
+                nc.scalar.copy(
+                    wd_bf[a][:, n0 : n0 + N // 2, :].rearrange("p (c i) t -> p c t i", i=LINE),
+                    wd_raw[a][:, :, n0 : n0 + N // 2].rearrange("p t (c i) -> p c t i", i=LINE),
                 )
 
-        def squares(b, a, c0, width, at=None):
+        def quantize_wd(a, at):
+            wd_w[a] = keep.tile([P, N], U32, name=f"wd_w{a}", align_bytes=64)
+            wd_s[a] = shared.tile([P, N], U8, name=f"wd_s{a}", offset=at, align_bytes=64)
+            for c0, c1 in ((0, HALF), (HALF, N)):
+                nc.vector.quantize_mx(
+                    out=wd_w[a][:, c0:c1].bitcast(FP8X4),
+                    scales=wd_s[a][:, c0:c1],
+                    in_=wd_bf[a][:, c0:c1, :].rearrange("p n t -> p (n t)"),
+                )
+
+        def squares(b, a, c0, width, banks, at=None):
             if at is None:
                 square[b, a, c0] = ring.tile([P, PACK, width], F32, name="square", bufs=SQUARE_BUFS)
             else:
                 square[b, a, c0] = shared.tile([P, PACK, width], F32, name=f"square{b}{a}{c0}", offset=at, align_bytes=64)
             per_bank = BANK // width
             cols = slice(c0, c0 + width)
-            for t0 in range(0, PACK, per_bank):
-                dots = psum.tile([P, per_bank, width], F32, name="dots")
+            for t0, bank in zip(range(0, PACK, per_bank), banks):
+                dots = psum.tile([P, per_bank, width], F32, name="dots", tag=f"bank{bank}")
                 for g in range(per_bank):
                     nc.tensor.matmul_mx(
                         out=dots[:, g, :],
@@ -241,10 +243,10 @@ def tile_list_handle_patch_deform_kernel(
         def tiles_per_bank(width):
             return min(BANK // width, WD_TILES)
 
-        def multiply(b, a, first, width, tile0, tag="prod", part=None):
+        def multiply(b, a, first, width, tile0, into=None, part=None):
             count = tiles_per_bank(width)
             if a == 0:
-                prod[b, first, tile0] = psum.tile([P, count, width], F32, name="prod", tag=tag)
+                prod[b, first, tile0] = psum.tile([P, count, width], F32, name="prod", tag=f"bank{into}")
             bank = prod[b, first, tile0]
             for g in range(count):
                 row_tile = tile0 + g
@@ -253,9 +255,9 @@ def tile_list_handle_patch_deform_kernel(
                 for c0 in range(lo, hi, step):
                     cols = slice(first + c0, first + c0 + step)
                     if row_tile < WD_TILES:
-                        picked_rows = slice(a * N + row_tile * P, a * N + (row_tile + 1) * P)
-                        weights = wd_q["words"][:, picked_rows].bitcast(FP8X4)
-                        weight_scales = wd_q["scales"][:, picked_rows]
+                        picked_rows = slice(row_tile * P, (row_tile + 1) * P)
+                        weights = wd_w[a][:, picked_rows].bitcast(FP8X4)
+                        weight_scales = wd_s[a][:, picked_rows]
                     else:
                         m = row_tile - WD_TILES
                         weights = w4_w[:, a, m * P // 2 : (m + 1) * P // 2].bitcast(U8).bitcast(FP4X4)
@@ -288,7 +290,9 @@ def tile_list_handle_patch_deform_kernel(
                 multiply(b, a, first, width, tile0)
             store(b, first, width, tile0, on_vector)
 
+        copy_qb_row(1)
         copy_qb_row(LAST)
+        make_base(1, 1)
         make_base(LAST, 0)
         make_base(LAST, 1)
         w4_w = keep.tile([P, PASSES, M // 2], I32, name="w4_w", tag="qb_row2", align_bytes=64)
@@ -296,9 +300,7 @@ def tile_list_handle_patch_deform_kernel(
         make_base(0, 0)
         make_base(0, 1)
         make_base(1, 0)
-        make_base(1, 1)
-        round_wd(0, False)
-        round_wd(1, False)
+        round_wd(0)
         gather_handle_scales(0)
         gather_handle_scales(1)
         gather_handle_words(0, "hand_w0")
@@ -307,62 +309,91 @@ def tile_list_handle_patch_deform_kernel(
         gather_vertex_scales(1, "vert_s1")
         gather_vertex_words(0, "vert_w0")
         gather_vertex_words(1, "vert_w1")
-        squares(0, 0, 0, BANK)
+        squares(0, 0, 0, BANK, (0, 1, 2, 3,))
         roots(0, 0, 0, BANK, 0)
-        squares(0, 1, 0, BANK)
-        roots(0, 1, 0, HALF, 6144)
-        roots(0, 1, HALF, HALF, 4096)
-        squares(1, 0, 0, BANK)
+        squares(0, 1, 0, BANK, (0, 1, 2, 3,))
+        roots(0, 1, 0, BANK, 4096)
+        round_wd(1)
+        squares(1, 0, 0, BANK, (0, 1, 2, 3,))
         quantize_z(0, 0, 0, BANK)
-        quantize_wd(0)
-        quantize_z(0, 1, 0, HALF)
-        quantize_z(0, 1, HALF, HALF)
-        squares(1, 1, 0, BANK, 7168)
+        quantize_z(0, 1, 0, BANK)
+        quantize_wd(0, 4096)
+        squares(1, 1, 0, BANK, (0, 1, 2, 3,), 7168)
         roots(1, 0, 0, BANK)
+        quantize_wd(1, 49152)
+        multiply(0, 0, 0, BANK, 3, 4)
+        multiply(0, 1, 0, BANK, 3)
+        multiply(0, 0, 0, BANK, 4, 5)
+        multiply(0, 1, 0, BANK, 4)
+        multiply(0, 0, 0, BANK, 5, 6)
+        multiply(0, 1, 0, BANK, 5)
+        multiply(0, 0, 0, BANK, 0, 7)
+        multiply(0, 1, 0, BANK, 0)
         quantize_z(1, 0, 0, BANK)
-        displace(0, 0, BANK, 3, False)
-        displace(0, 0, BANK, 4, False)
-        displace(0, 0, BANK, 5, False)
+        store(0, 0, BANK, 3, False)
+        multiply(0, 0, 0, BANK, 1, 4)
+        multiply(0, 1, 0, BANK, 1)
+        store(0, 0, BANK, 4, False)
+        multiply(0, 0, 0, BANK, 2, 5)
+        multiply(0, 1, 0, BANK, 2)
+        store(0, 0, BANK, 5, False)
         roots(1, 1, 0, BANK, 16384)
         gather_vertex_scales(2, "base111")
         gather_vertex_words(2, "base112")
-        displace(0, 0, BANK, 0, False)
-        displace(0, 0, BANK, 1, False)
-        displace(0, 0, BANK, 2, False)
+        multiply(1, 0, 0, BANK, 0, 0)
+        multiply(1, 0, 0, BANK, 1, 1)
+        multiply(1, 0, 0, BANK, 2, 2)
+        multiply(1, 0, 0, BANK, 3, 3)
+        store(0, 0, BANK, 0, False)
+        store(0, 0, BANK, 1, False)
+        store(0, 0, BANK, 2, False)
         quantize_z(1, 1, 0, BANK)
-        squares(2, 0, 0, HALF, 14336)
-        squares(2, 1, 0, HALF, 18432)
-        displace(1, 0, BANK, 0, False)
+        squares(2, 0, 0, HALF, (6, 7,), 14336)
+        multiply(1, 1, 0, BANK, 0)
+        multiply(1, 1, 0, BANK, 1)
+        squares(2, 1, 0, HALF, (4, 5,), 18432)
+        multiply(1, 1, 0, BANK, 2)
+        multiply(1, 1, 0, BANK, 3)
+        store(1, 0, BANK, 0, False)
+        store(1, 0, BANK, 1, False)
         roots(2, 0, 0, HALF)
-        displace(1, 0, BANK, 1, True)
-        squares(2, 0, HALF, HALF)
-        displace(1, 0, BANK, 2, False)
+        squares(2, 0, HALF, HALF, (6, 7,))
+        multiply(1, 0, 0, BANK, 4, 0)
+        multiply(1, 1, 0, BANK, 4)
+        multiply(1, 0, 0, BANK, 5, 1)
+        multiply(1, 1, 0, BANK, 5)
+        store(1, 0, BANK, 2, False)
         roots(2, 1, 0, HALF)
         quantize_z(2, 0, 0, HALF)
-        displace(1, 0, BANK, 3, True)
+        store(1, 0, BANK, 3, True)
         quantize_z(2, 1, 0, HALF)
-        squares(2, 1, HALF, P)
-        squares(2, 1, HALF + P, P)
-        displace(1, 0, BANK, 4, False)
+        squares(2, 1, HALF, HALF, (4, 5,))
         roots(2, 0, HALF, HALF)
-        displace(1, 0, BANK, 5, False)
+        store(1, 0, BANK, 4, False)
         quantize_z(2, 0, HALF, HALF)
-        displace(2, 0, HALF, 0, True)
+        multiply(2, 0, 0, HALF, 0, 2)
+        multiply(2, 1, 0, HALF, 0)
+        multiply(2, 0, 0, HALF, 2, 3)
+        multiply(2, 1, 0, HALF, 2)
+        multiply(2, 0, 0, HALF, 4, 6)
+        multiply(2, 1, 0, HALF, 4)
         roots(2, 1, HALF, P)
         roots(2, 1, HALF + P, P)
+        store(1, 0, BANK, 5, True)
         quantize_z(2, 1, HALF, P)
-        multiply(2, 0, HALF, HALF, 0, "dots")
-        multiply(2, 0, HALF, HALF, 2, "dots")
-        multiply(2, 0, HALF, HALF, 4, "dots")
-        displace(2, 0, HALF, 2, True)
-        quantize_z(2, 1, HALF + P, P)
-        displace(2, 0, HALF, 4, False)
+        multiply(2, 0, HALF, HALF, 0, 7)
+        multiply(2, 0, HALF, HALF, 2, 4)
+        multiply(2, 0, HALF, HALF, 4, 5)
         multiply(LAST, 1, HALF, HALF, 0, part=(0, P))
         multiply(LAST, 1, HALF, HALF, 2, part=(0, P))
         multiply(LAST, 1, HALF, HALF, 4, part=(0, P))
+        store(2, 0, HALF, 0, True)
+        quantize_z(2, 1, HALF + P, P)
+        store(2, 0, HALF, 2, False)
         multiply(LAST, 1, HALF, HALF, 0, part=(P, HALF))
-        store(2, HALF, HALF, 0, False)
         multiply(LAST, 1, HALF, HALF, 2, part=(P, HALF))
-        store(2, HALF, HALF, 2, True)
         multiply(LAST, 1, HALF, HALF, 4, part=(P, HALF))
+        store(2, 0, HALF, 4, False)
+        store(2, HALF, HALF, 0, False)
+        store(2, HALF, HALF, 2, True)
         store(2, HALF, HALF, 4, False)

@@ -189,9 +189,9 @@ def tile_list_handle_patch_deform_kernel(
 
         def squares(b, a, c0, width, banks, at=None):
             if at is None:
-                square[b, a, c0] = ring.tile([P, PACK, width], F32, name="square", bufs=SQUARE_BUFS)
+                square[b, a, c0] = ring.tile([P, width // LINE, PACK, LINE], F32, name="square", bufs=SQUARE_BUFS)
             else:
-                square[b, a, c0] = shared.tile([P, PACK, width], F32, name=f"square{b}{a}{c0}", offset=at, align_bytes=64)
+                square[b, a, c0] = shared.tile([P, width // LINE, PACK, LINE], F32, name=f"square{b}{a}{c0}", offset=at, align_bytes=64)
             per_bank = BANK // width
             cols = slice(c0, c0 + width)
             for t0, bank in zip(range(0, PACK, per_bank), banks):
@@ -209,10 +209,10 @@ def tile_list_handle_patch_deform_kernel(
                 for g in range(per_bank):
                     t = t0 + g
                     nc.vector.scalar_tensor_tensor(
-                        square[b, a, c0][:, t, :],
-                        dots[:, g, :],
+                        square[b, a, c0][:, :, t, :],
+                        dots[:, g, :].rearrange("p (c i) -> p c i", i=LINE),
                         hw2_m2[:, a, t : t + 1],
-                        base[b, a, t][:, cols],
+                        base[b, a, t][:, cols].rearrange("p (c i) -> p c i", i=LINE),
                         ALU.mult,
                         ALU.add,
                     )
@@ -225,7 +225,7 @@ def tile_list_handle_patch_deform_kernel(
             s0 = max(c for (bb, aa, c) in square if (bb, aa) == (b, a) and c <= c0)
             nc.scalar.activation(
                 z_bf[b, a, c0][:].rearrange("p (c i) t -> p c t i", i=LINE),
-                square[b, a, s0][:, :, c0 - s0 : c0 - s0 + width].rearrange("p t (c i) -> p c t i", i=LINE),
+                square[b, a, s0][:, (c0 - s0) // LINE : (c0 - s0 + width) // LINE],
                 ACT.Sqrt,
             )
 

@@ -56,9 +56,9 @@ def tile_list_handle_patch_deform_kernel(
         list2 = keep.tile([P, S2 // 16], U16, name="list2")
         tab_s = keep.tile([P, T // 4], I32, name="tab_s", align_bytes=64)
         tab2_s = keep.tile([P, T2 // 4], I32, name="tab2_s", align_bytes=64)
-        qb_col = keep.tile([P, BLOCKS, PACK], F32, name="qb_col", tag="after_qb", align_bytes=64)
+        qb_col = shared.tile([P, BLOCKS, PACK], F32, name="qb_col", offset=2048, align_bytes=64)
         hw_col = keep.tile([P, PASSES, PACK], F32, name="hw_col", tag="after_hw", align_bytes=64)
-        qa_col = shared.tile([P, PASSES, PACK], F32, name="qa_col", offset=2048, align_bytes=64)
+        qa_col = keep.tile([P, PASSES, PACK], F32, name="qa_col", tag="after_qa", align_bytes=64)
         zeros = keep.tile([P, P], F32, name="zeros", tag="after_zeros", align_bytes=64)
         ident = keep.tile([P, P], F32, name="ident", tag="after_ident", align_bytes=64)
         one = keep.tile([P, 1], F32, name="one")
@@ -106,8 +106,8 @@ def tile_list_handle_patch_deform_kernel(
             qb_bank[b] = spread
 
         wd_raw = [
-            shared.tile([P, PACK, N], F32, name="wd_raw0", offset=2048, align_bytes=64),
-            keep.tile([P, PACK, N], F32, name="wd_raw1", tag="after_qb", align_bytes=64),
+            keep.tile([P, PACK, N], F32, name="wd_raw0", tag="after_qa", align_bytes=64),
+            shared.tile([P, PACK, N], F32, name="wd_raw1", offset=2048, align_bytes=64),
         ]
         for a in range(PASSES):
             rows = wd[a * P * PACK : (a + 1) * P * PACK, :]
@@ -177,9 +177,9 @@ def tile_list_handle_patch_deform_kernel(
                     wd_raw[a][:, :, n0 : n0 + N // 2].rearrange("p t (c i) -> p c t i", i=LINE),
                 )
 
-        def quantize_wd(a, at):
+        def quantize_wd(a, slot):
             wd_w[a] = keep.tile([P, N], U32, name=f"wd_w{a}", align_bytes=64)
-            wd_s[a] = shared.tile([P, N], U8, name=f"wd_s{a}", offset=at, align_bytes=64)
+            wd_s[a] = keep.tile([P, N], U8, name=f"wd_s{a}", tag=slot, align_bytes=64)
             for c0, c1 in ((0, HALF), (HALF, N)):
                 nc.vector.quantize_mx(
                     out=wd_w[a][:, c0:c1].bitcast(FP8X4),
@@ -301,32 +301,33 @@ def tile_list_handle_patch_deform_kernel(
         make_base(0, 1)
         make_base(1, 0)
         round_wd(0)
+        round_wd(1)
         gather_handle_scales(0)
         gather_handle_scales(1)
         gather_handle_words(0, "hand_w0")
         gather_handle_words(1, "hand_w1")
         gather_vertex_scales(0, "vert_s0")
         gather_vertex_scales(1, "vert_s1")
+        gather_vertex_scales(2, "vert_s2")
         gather_vertex_words(0, "vert_w0")
         gather_vertex_words(1, "vert_w1")
         squares(0, 0, 0, BANK, (0, 1, 2, 3,))
         roots(0, 0, 0, BANK, 0)
         squares(0, 1, 0, BANK, (0, 1, 2, 3,))
         roots(0, 1, 0, BANK, 4096)
-        round_wd(1)
         squares(1, 0, 0, BANK, (0, 1, 2, 3,))
         quantize_z(0, 0, 0, BANK)
         quantize_z(0, 1, 0, BANK)
-        quantize_wd(0, 4096)
         squares(1, 1, 0, BANK, (0, 1, 2, 3,), 7168)
         roots(1, 0, 0, BANK)
-        quantize_wd(1, 49152)
         multiply(0, 0, 0, BANK, 3, 4)
         multiply(0, 1, 0, BANK, 3)
         multiply(0, 0, 0, BANK, 4, 5)
         multiply(0, 1, 0, BANK, 4)
         multiply(0, 0, 0, BANK, 5, 6)
         multiply(0, 1, 0, BANK, 5)
+        quantize_wd(0, "base110")
+        quantize_wd(1, "base111")
         multiply(0, 0, 0, BANK, 0, 7)
         multiply(0, 1, 0, BANK, 0)
         quantize_z(1, 0, 0, BANK)
@@ -338,7 +339,6 @@ def tile_list_handle_patch_deform_kernel(
         multiply(0, 1, 0, BANK, 2)
         store(0, 0, BANK, 5, False)
         roots(1, 1, 0, BANK, 16384)
-        gather_vertex_scales(2, "base111")
         gather_vertex_words(2, "base112")
         multiply(1, 0, 0, BANK, 0, 0)
         multiply(1, 0, 0, BANK, 1, 1)
@@ -381,19 +381,19 @@ def tile_list_handle_patch_deform_kernel(
         roots(2, 1, HALF + P, P)
         store(1, 0, BANK, 5, True)
         quantize_z(2, 1, HALF, P)
-        multiply(2, 0, HALF, HALF, 0, 7)
-        multiply(2, 0, HALF, HALF, 2, 4)
-        multiply(2, 0, HALF, HALF, 4, 5)
-        multiply(LAST, 1, HALF, HALF, 0, part=(0, P))
-        multiply(LAST, 1, HALF, HALF, 2, part=(0, P))
-        multiply(LAST, 1, HALF, HALF, 4, part=(0, P))
+        multiply(2, 0, HALF, P, 0, 7)
+        multiply(2, 0, HALF, P, 3, 4)
+        multiply(2, 1, HALF, P, 0)
+        multiply(2, 1, HALF, P, 3)
+        multiply(2, 0, HALF + P, P, 0, 5)
+        multiply(2, 0, HALF + P, P, 3, 0)
         store(2, 0, HALF, 0, True)
         quantize_z(2, 1, HALF + P, P)
         store(2, 0, HALF, 2, False)
-        multiply(LAST, 1, HALF, HALF, 0, part=(P, HALF))
-        multiply(LAST, 1, HALF, HALF, 2, part=(P, HALF))
-        multiply(LAST, 1, HALF, HALF, 4, part=(P, HALF))
+        multiply(2, 1, HALF + P, P, 0)
+        multiply(2, 1, HALF + P, P, 3)
         store(2, 0, HALF, 4, False)
-        store(2, HALF, HALF, 0, False)
-        store(2, HALF, HALF, 2, True)
-        store(2, HALF, HALF, 4, False)
+        store(2, HALF, P, 0, True)
+        store(2, HALF, P, 3, False)
+        store(2, HALF + P, P, 0, True)
+        store(2, HALF + P, P, 3, False)

@@ -26,7 +26,7 @@ LAST = BLOCKS - 1
 LIST_COLS = BANK // 16
 ROW_TILES = (N + M) // P
 WD_TILES = N // P
-LINE = 4
+LINE = 2
 TAB2_ROW = 4
 LAST_PIECES = [(0, HALF), (HALF, P), (HALF + P, P)]
 PSUM_BUFS = 1
@@ -189,9 +189,9 @@ def tile_list_handle_patch_deform_kernel(
 
         def squares(b, a, c0, width, banks, at=None):
             if at is None:
-                square[b, a, c0] = ring.tile([P, width // LINE, PACK, LINE], F32, name="square", bufs=SQUARE_BUFS)
+                square[b, a, c0] = ring.tile([P, PACK, width], F32, name="square", bufs=SQUARE_BUFS)
             else:
-                square[b, a, c0] = shared.tile([P, width // LINE, PACK, LINE], F32, name=f"square{b}{a}{c0}", offset=at, align_bytes=64)
+                square[b, a, c0] = shared.tile([P, PACK, width], F32, name=f"square{b}{a}{c0}", offset=at, align_bytes=64)
             per_bank = BANK // width
             cols = slice(c0, c0 + width)
             for t0, bank in zip(range(0, PACK, per_bank), banks):
@@ -209,10 +209,10 @@ def tile_list_handle_patch_deform_kernel(
                 for g in range(per_bank):
                     t = t0 + g
                     nc.vector.scalar_tensor_tensor(
-                        square[b, a, c0][:, :, t, :],
-                        dots[:, g, :].rearrange("p (c i) -> p c i", i=LINE),
+                        square[b, a, c0][:, t, :],
+                        dots[:, g, :],
                         hw2_m2[:, a, t : t + 1],
-                        base[b, a, t][:, cols].rearrange("p (c i) -> p c i", i=LINE),
+                        base[b, a, t][:, cols],
                         ALU.mult,
                         ALU.add,
                     )
@@ -225,7 +225,7 @@ def tile_list_handle_patch_deform_kernel(
             s0 = max(c for (bb, aa, c) in square if (bb, aa) == (b, a) and c <= c0)
             nc.scalar.activation(
                 z_bf[b, a, c0][:].rearrange("p (c i) t -> p c t i", i=LINE),
-                square[b, a, s0][:, (c0 - s0) // LINE : (c0 - s0 + width) // LINE],
+                square[b, a, s0][:, :, c0 - s0 : c0 - s0 + width].rearrange("p t (c i) -> p c t i", i=LINE),
                 ACT.Sqrt,
             )
 

@@ -56,7 +56,7 @@ def tile_list_handle_patch_deform_kernel(
         list2 = keep.tile([P, S2 // 16], U16, name="list2")
         tab_s = keep.tile([P, T // 4], I32, name="tab_s", align_bytes=64)
         tab2_s = keep.tile([P, T2 // 4], I32, name="tab2_s", align_bytes=64)
-        qb_col = shared.tile([P, BLOCKS, PACK], F32, name="qb_col", offset=2048, align_bytes=64)
+        qb_col = shared.tile([P, BLOCKS, PACK], F32, name="qb_col", offset=24576, align_bytes=64)
         hw_col = keep.tile([P, PASSES, PACK], F32, name="hw_col", tag="after_hw", align_bytes=64)
         qa_col = keep.tile([P, PASSES, PACK], F32, name="qa_col", tag="after_qa", align_bytes=64)
         zeros = keep.tile([P, P], F32, name="zeros", tag="after_zeros", align_bytes=64)
@@ -64,13 +64,14 @@ def tile_list_handle_patch_deform_kernel(
         one = keep.tile([P, 1], F32, name="one")
         root_of_one = keep.tile([P, 1], F32, name="root_of_one")
 
-        nc.gpsimd.dma_start(out=qb_col[:], in_=qb.rearrange("(b p c) -> p b c", p=P, c=PACK))
-        nc.scalar.dma_start(out=hw_col[:], in_=hw.rearrange("(a p t) -> p a t", p=P, t=PACK))
-        nc.scalar.dma_start(out=qa_col[:], in_=qa.rearrange("(a p t) -> p a t", p=P, t=PACK))
-        nc.vector.memset(tab_s[:], 0)
+        nc.sync.dma_start(list1[:], offs)
+        nc.sync.dma_start(out=hw_col[:], in_=hw.rearrange("(a p t) -> p a t", p=P, t=PACK))
+        nc.sync.dma_start(out=qa_col[:], in_=qa.rearrange("(a p t) -> p a t", p=P, t=PACK))
+        nc.gpsimd.memset(tab_s[:, T // 8 :], 0)
+        nc.gpsimd.memset(zeros[:], 0.0)
+        nc.vector.memset(tab_s[:, : T // 8], 0)
         nc.vector.memset(one[:], 1.0)
         nc.scalar.activation(root_of_one[:], one[:], ACT.Sqrt)
-        nc.vector.memset(zeros[:], 0.0)
         nc.vector.memset(tab2_s[:], 0)
         nc.gpsimd.affine_select(
             out=ident[:],
@@ -81,20 +82,20 @@ def tile_list_handle_patch_deform_kernel(
             pattern=[[-1, P]],
             channel_multiplier=1,
         )
+        nc.gpsimd.dma_start(out=qb_col[:], in_=qb.rearrange("(b p c) -> p b c", p=P, c=PACK))
 
-        nc.sync.dma_start(list1[:], offs)
-        nc.sync.dma_start(list2[:], offs2)
         load_scale_rows(nc.sync, tab_s, tab_scales[0].bitcast(I32).rearrange("(q r) w -> r q w", r=4), 0)
         tab_w = keep.tile([P, T], I32, name="tab_w", tag="after_zeros", align_bytes=64)
         nc.sync.dma_start(out=tab_w[:], in_=tab_words[0].rearrange("p t i -> p (t i)").bitcast(I32))
+        nc.sync.dma_start(list2[:], offs2)
         load_scale_rows(nc.sync, tab2_s, tab2_scales[0].bitcast(I32).rearrange("(q r) w -> r q w", r=4), TAB2_ROW)
 
         hw2 = keep.tile([P, PASSES, PACK], F32, name="hw2")
         hw2_qa = keep.tile([P, PASSES, PACK], F32, name="hw2_qa")
-        hw2_m2 = keep.tile([P, PASSES, PACK], F32, name="hw2_m2")
-        nc.vector.tensor_tensor(hw2[:], hw_col[:], hw_col[:], ALU.mult)
-        nc.vector.scalar_tensor_tensor(hw2_m2[:], hw_col[:], -2.0, hw_col[:], ALU.mult, ALU.mult)
-        nc.vector.tensor_tensor(hw2_qa[:], hw2[:], qa_col[:], ALU.mult)
+        hw2_qa_s = keep.tile([P, PASSES, PACK], F32, name="hw2_qa_s", tag="after_bases", align_bytes=64)
+        nc.gpsimd.tensor_tensor(hw2[:], hw_col[:], hw_col[:], ALU.mult)
+        nc.gpsimd.tensor_tensor(hw2_qa_s[:], hw2[:], qa_col[:], ALU.mult)
+        nc.gpsimd.tensor_tensor(hw2_qa[:], hw2[:], qa_col[:], ALU.mult)
         tab2_w = keep.tile([P, T2], I32, name="tab2_w", tag="after_hw", align_bytes=64)
         nc.sync.dma_start(out=tab2_w[:], in_=tab2_words[0].rearrange("p t i -> p (t i)").bitcast(I32))
 
@@ -107,7 +108,7 @@ def tile_list_handle_patch_deform_kernel(
 
         wd_raw = [
             keep.tile([P, PACK, N], F32, name="wd_raw0", tag="after_qa", align_bytes=64),
-            shared.tile([P, PACK, N], F32, name="wd_raw1", offset=2048, align_bytes=64),
+            shared.tile([P, PACK, N], F32, name="wd_raw1", offset=24576, align_bytes=64),
         ]
         for a in range(PASSES):
             rows = wd[a * P * PACK : (a + 1) * P * PACK, :]
@@ -124,10 +125,10 @@ def tile_list_handle_patch_deform_kernel(
             qb_row[b] = keep.tile([P, BANK], F32, name=f"qb_row{b}", align_bytes=64)
             nc.scalar.copy(qb_row[b][:].rearrange("p (n c) -> p n c", c=PACK), qb_bank[b][:].rearrange("p c n -> p n c"))
 
-        def make_base(b, a):
-            for t in range(PACK):
+        def make_base(b, a, ts, on_gpsimd):
+            for t in ts:
                 tile = keep.tile([P, BANK], F32, name=f"base{b}{a}{t}", tag=f"base{b}{a}{t}", align_bytes=64)
-                if (b, a) >= (1, 1):
+                if on_gpsimd:
                     nc.gpsimd.tensor_scalar(
                         tile[:], qb_row[b][:], hw2[:, a, t : t + 1], hw2_qa[:, a, t : t + 1], ALU.mult, ALU.add
                     )
@@ -136,7 +137,7 @@ def tile_list_handle_patch_deform_kernel(
                         tile[:].rearrange("p (n c) -> p n c", c=PACK),
                         qb_bank[b][:].rearrange("p c n -> p n c"),
                         ACT.Identity,
-                        bias=hw2_qa[:, a, t : t + 1],
+                        bias=hw2_qa_s[:, a, t : t + 1],
                         scale=hw2[:, a, t : t + 1],
                     )
                 base[b, a, t] = tile
@@ -153,10 +154,12 @@ def tile_list_handle_patch_deform_kernel(
             hand_w[a] = keep.tile([P, PACK, P], U32, name=f"hand_w{a}", tag=slot, align_bytes=64)
             nc.vector.tensor_copy(hand_w[a][:].rearrange("p t m -> p m t"), tab_w[:].bitcast(U32).indirect(entries))
 
-        def gather_vertex_scales(b, slot):
-            vert_s[b] = keep.tile([P, BANK], U8, name=f"vert_s{b}", tag=slot, align_bytes=64)
-            entries = list2[:, b * LIST_COLS : (b + 1) * LIST_COLS]
-            nc.vector.tensor_copy(vert_s[b][:], tab2_s[:].bitcast(U8).indirect(entries))
+        def gather_vertex_scales(b0, b1, slot):
+            tile = keep.tile([P, (b1 - b0) * BANK], U8, name=f"vert_s{b0}", tag=slot, align_bytes=64)
+            entries = list2[:, b0 * LIST_COLS : b1 * LIST_COLS]
+            nc.vector.tensor_copy(tile[:], tab2_s[:].bitcast(U8).indirect(entries))
+            for b in range(b0, b1):
+                vert_s[b] = tile[:, (b - b0) * BANK : (b - b0 + 1) * BANK]
 
         def gather_vertex_words(b, slot, at=None):
             if at is None:
@@ -172,9 +175,13 @@ def tile_list_handle_patch_deform_kernel(
             else:
                 wd_bf[a] = shared.tile([P, N, PACK], BF16, name=f"wd_bf{a}", offset=at, align_bytes=64)
             for n0 in range(0, N, N // 2):
-                nc.scalar.copy(
-                    wd_bf[a][:, n0 : n0 + N // 2, :].rearrange("p (c i) t -> p c t i", i=LINE),
-                    wd_raw[a][:, :, n0 : n0 + N // 2].rearrange("p t (c i) -> p c t i", i=LINE),
+                nc.gpsimd.tensor_scalar(
+                    wd_bf[a][:, n0 : n0 + N // 2, :],
+                    wd_raw[a][:, :, n0 : n0 + N // 2].rearrange("p t n -> p n t"),
+                    1.0,
+                    0.0,
+                    ALU.mult,
+                    ALU.add,
                 )
 
         def quantize_wd(a, slot):
@@ -292,23 +299,24 @@ def tile_list_handle_patch_deform_kernel(
 
         copy_qb_row(1)
         copy_qb_row(LAST)
-        make_base(1, 1)
-        make_base(LAST, 0)
-        make_base(LAST, 1)
-        w4_w = keep.tile([P, PASSES, M // 2], I32, name="w4_w", tag="qb_row2", align_bytes=64)
-        nc.sync.dma_start(out=w4_w[:], in_=w4_words.bitcast(I32).rearrange("a p w -> p a w"))
-        make_base(0, 0)
-        make_base(0, 1)
-        make_base(1, 0)
+        make_base(1, 1, range(PACK), True)
         round_wd(0)
         round_wd(1)
+        make_base(LAST, 0, range(PACK), True)
+        w4_w = keep.tile([P, PASSES, M // 2], I32, name="w4_w", tag="qb_row1", align_bytes=64)
+        nc.sync.dma_start(out=w4_w[:], in_=w4_words.bitcast(I32).rearrange("a p w -> p a w"))
+        make_base(0, 0, range(PACK), False)
+        make_base(0, 1, range(PACK), False)
+        make_base(1, 0, range(PACK), False)
+        make_base(LAST, 1, (0, 1), False)
+        hw2_m2 = keep.tile([P, PASSES, PACK], F32, name="hw2_m2")
+        nc.scalar.activation(hw2_m2[:], hw2[:], ACT.Copy, scale=-2.0)
+        make_base(LAST, 1, (2, 3), False)
         gather_handle_scales(0)
         gather_handle_scales(1)
+        gather_vertex_scales(0, BLOCKS, "vert_s0")
         gather_handle_words(0, "hand_w0")
         gather_handle_words(1, "hand_w1")
-        gather_vertex_scales(0, "vert_s0")
-        gather_vertex_scales(1, "vert_s1")
-        gather_vertex_scales(2, "vert_s2")
         gather_vertex_words(0, "vert_w0")
         gather_vertex_words(1, "vert_w1")
         squares(0, 0, 0, BANK, (0, 1, 2, 3,))

@@ -119,6 +119,7 @@ def tile_list_handle_patch_deform_kernel(
 
         base, hand_w, hand_s, vert_w, vert_s = {}, {}, {}, {}, {}
         wd_bf, wd_w, wd_s = {}, {}, {}
+        listed_w = {}
         square, z_bf, z_w, z_s, qb_row, prod = {}, {}, {}, {}, {}, {}
 
         def copy_qb_row(b):
@@ -150,9 +151,16 @@ def tile_list_handle_patch_deform_kernel(
             nc.vector.tensor_copy(hand_s[a][:], picked[:].rearrange("p m t -> p t m"))
 
         def gather_handle_words(a, slot):
+            listed_w[a] = keep.tile([P, P, PACK], U32, name=f"listed_w{a}", align_bytes=64)
             entries = list1[:, a * LIST_COLS : (a + 1) * LIST_COLS]
-            hand_w[a] = keep.tile([P, PACK, P], U32, name=f"hand_w{a}", tag=slot, align_bytes=64)
-            nc.vector.tensor_copy(hand_w[a][:].rearrange("p t m -> p m t"), tab_w[:].bitcast(U32).indirect(entries))
+            nc.vector.tensor_copy(listed_w[a][:].rearrange("p m t -> p (m t)"), tab_w[:].bitcast(U32).indirect(entries))
+
+        def part_handle_words(a):
+            hand_w[a] = keep.tile([P, PACK, P], U32, name=f"hand_w{a}", align_bytes=64)
+            nc.vector.tensor_copy(
+                hand_w[a][:].rearrange("p t (c i) -> p c t i", i=PACK),
+                listed_w[a][:].rearrange("p (c i) t -> p c t i", i=PACK),
+            )
 
         def gather_vertex_scales(b0, b1, slot):
             tile = keep.tile([P, (b1 - b0) * BANK], U8, name=f"vert_s{b0}", tag=slot, align_bytes=64)
@@ -317,6 +325,8 @@ def tile_list_handle_patch_deform_kernel(
         gather_vertex_scales(0, BLOCKS, "vert_s0")
         gather_handle_words(0, "hand_w0")
         gather_handle_words(1, "hand_w1")
+        part_handle_words(0)
+        part_handle_words(1)
         gather_vertex_words(0, "vert_w0")
         gather_vertex_words(1, "vert_w1")
         squares(0, 0, 0, BANK, (0, 1, 2, 3,))

@@ -56,7 +56,8 @@ def tile_list_handle_patch_deform_kernel(
         list2 = keep.tile([P, S2 // 16], U16, name="list2")
         tab_s = keep.tile([P, T // 4], I32, name="tab_s", align_bytes=64)
         tab2_s = keep.tile([P, T2 // 4], I32, name="tab2_s", align_bytes=64)
-        qb_col = shared.tile([P, BLOCKS, PACK], F32, name="qb_col", offset=24576, align_bytes=64)
+        qb_slot = shared.tile([P, 8, PACK], F32, name="qb_col", offset=24576 + 3072 - 64, align_bytes=64)
+        qb_col = qb_slot[:, :BLOCKS, :]
         hw_col = keep.tile([P, PASSES, PACK], F32, name="hw_col", tag="after_hw", align_bytes=64)
         qa_col = keep.tile([P, PASSES, PACK], F32, name="qa_col", tag="after_qa", align_bytes=64)
         zeros = keep.tile([P, P], F32, name="zeros", tag="after_zeros", align_bytes=64)
@@ -82,7 +83,7 @@ def tile_list_handle_patch_deform_kernel(
             pattern=[[-1, P]],
             channel_multiplier=1,
         )
-        nc.gpsimd.dma_start(out=qb_col[:], in_=qb.rearrange("(b p c) -> p b c", p=P, c=PACK))
+        nc.gpsimd.dma_start(out=qb_col, in_=qb.rearrange("(b p c) -> p b c", p=P, c=PACK))
 
         load_scale_rows(nc.sync, tab_s, tab_scales[0].bitcast(I32).rearrange("(q r) w -> r q w", r=4), 0)
         tab_w = keep.tile([P, T], I32, name="tab_w", tag="after_zeros", align_bytes=64)
@@ -106,13 +107,14 @@ def tile_list_handle_patch_deform_kernel(
                 nc.tensor.transpose(spread[:, c, :], qb_col[:, b, c : c + 1].to_broadcast([P, P]), ident[:])
             qb_bank[b] = spread
 
-        wd_raw = [
-            keep.tile([P, PACK, N], F32, name="wd_raw0", tag="after_qa", align_bytes=64),
-            shared.tile([P, PACK, N], F32, name="wd_raw1", offset=24576, align_bytes=64),
-        ]
-        for a in range(PASSES):
-            rows = wd[a * P * PACK : (a + 1) * P * PACK, :]
-            nc.sync.dma_start(out=wd_raw[a][:], in_=rows.rearrange("(p t) n -> p t n", t=PACK))
+        wd_raw0 = keep.tile([P, PACK, N], F32, name="wd_raw0", tag="after_qa", align_bytes=64)
+        nc.sync.dma_start(out=wd_raw0[:], in_=wd[: P * PACK, :].rearrange("(p t) n -> p t n", t=PACK))
+        wd_raw1 = []
+        for h in range(2):
+            half = shared.tile([P, PACK, N // 2], F32, name=f"wd_raw1{h}", offset=24576 + 3072 * h, align_bytes=64)
+            rows = wd[P * PACK :, h * N // 2 : (h + 1) * N // 2]
+            nc.sync.dma_start(out=half[:], in_=rows.rearrange("(p t) n -> p t n", t=PACK))
+            wd_raw1.append(half)
         w4_s = keep.tile([P, PASSES, M // 4], I32, name="w4_s", tag="after_ident", align_bytes=64)
         nc.gpsimd.memset(w4_s[:], 0)
         load_scale_rows(nc.sync, w4_s, w4_scales.bitcast(I32).rearrange("a (q r) w -> r q a w", r=4), 0)
@@ -177,20 +179,18 @@ def tile_list_handle_patch_deform_kernel(
             entries = list2[:, b * LIST_COLS : (b + 1) * LIST_COLS]
             nc.vector.tensor_copy(vert_w[b][:], tab2_w[:].bitcast(U32).indirect(entries))
 
-        def round_wd(a, at=None):
-            if at is None:
-                wd_bf[a] = keep.tile([P, N, PACK], BF16, name=f"wd_bf{a}", align_bytes=64)
-            else:
-                wd_bf[a] = shared.tile([P, N, PACK], BF16, name=f"wd_bf{a}", offset=at, align_bytes=64)
-            for n0 in range(0, N, N // 2):
-                nc.gpsimd.tensor_scalar(
-                    wd_bf[a][:, n0 : n0 + N // 2, :],
-                    wd_raw[a][:, :, n0 : n0 + N // 2].rearrange("p t n -> p n t"),
-                    1.0,
-                    0.0,
-                    ALU.mult,
-                    ALU.add,
-                )
+        def round_wd(a):
+            wd_bf[a] = keep.tile([P, N, PACK], BF16, name=f"wd_bf{a}", align_bytes=64)
+            for h in range(2):
+                cols = slice(h * N // 2, (h + 1) * N // 2)
+                if a == 0:
+                    raw = wd_raw0[:, :, cols].rearrange("p t n -> p n t")
+                    nc.gpsimd.tensor_scalar(wd_bf[a][:, cols, :], raw, 1.0, 0.0, ALU.mult, ALU.add)
+                else:
+                    nc.scalar.copy(
+                        wd_bf[a][:, cols, :].rearrange("p (c i) t -> p c t i", i=LINE),
+                        wd_raw1[h][:].rearrange("p t (c i) -> p c t i", i=LINE),
+                    )
 
         def quantize_wd(a, slot):
             wd_w[a] = keep.tile([P, N], U32, name=f"wd_w{a}", align_bytes=64)
@@ -308,9 +308,9 @@ def tile_list_handle_patch_deform_kernel(
         copy_qb_row(1)
         copy_qb_row(LAST)
         make_base(1, 1, range(PACK), True)
-        round_wd(0)
-        round_wd(1)
         make_base(LAST, 0, range(PACK), True)
+        make_base(LAST, 1, (3,), True)
+        round_wd(0)
         w4_w = keep.tile([P, PASSES, M // 2], I32, name="w4_w", tag="qb_row1", align_bytes=64)
         nc.sync.dma_start(out=w4_w[:], in_=w4_words.bitcast(I32).rearrange("a p w -> p a w"))
         make_base(0, 0, range(PACK), False)
@@ -319,7 +319,8 @@ def tile_list_handle_patch_deform_kernel(
         make_base(LAST, 1, (0, 1), False)
         hw2_m2 = keep.tile([P, PASSES, PACK], F32, name="hw2_m2")
         nc.scalar.activation(hw2_m2[:], hw2[:], ACT.Copy, scale=-2.0)
-        make_base(LAST, 1, (2, 3), False)
+        make_base(LAST, 1, (2,), False)
+        round_wd(1)
         gather_handle_scales(0)
         gather_handle_scales(1)
         gather_vertex_scales(0, BLOCKS, "vert_s0")
@@ -330,7 +331,7 @@ def tile_list_handle_patch_deform_kernel(
         gather_vertex_words(0, "vert_w0")
         gather_vertex_words(1, "vert_w1")
         squares(0, 0, 0, BANK, (0, 1, 2, 3,))
-        roots(0, 0, 0, BANK, 0)
+        roots(0, 0, 0, BANK, 24576)
         squares(0, 1, 0, BANK, (0, 1, 2, 3,))
         roots(0, 1, 0, BANK, 4096)
         squares(1, 0, 0, BANK, (0, 1, 2, 3,))

from contextlib import ExitStack

import concourse.mybir as mybir

K, T, S, T2, S2, N, M = 512, 2048, 1024, 4096, 1536, 384, 384
FLOPS = 2 * K * S * S2 + 2 * S * (N + M) * S2

F32 = mybir.dt.float32
BF16 = mybir.dt.bfloat16
I32 = mybir.dt.int32
U32 = mybir.dt.uint32
U16 = mybir.dt.uint16
U8 = mybir.dt.uint8
FP8X4 = mybir.dt.float8_e4m3fn_x4
FP4X4 = mybir.dt.float4_e2m1fn_x4
ALU = mybir.AluOpType
ACT = mybir.ActivationFunctionType

P = 128
PACK = 4
BANK = 512
HALF = BANK // 2
PASSES = S // (P * PACK)
BLOCKS = S2 // BANK
LAST = BLOCKS - 1
LIST_COLS = BANK // 16
ROW_TILES = (N + M) // P
WD_TILES = N // P
LINE = 2
TAB2_ROW = 4
LAST_PIECES = [(0, HALF), (HALF, P), (HALF + P, P)]
PSUM_BUFS = 1
RING_BUFS = 3
SQUARE_BUFS = 3
ROUNDED_BUFS = 3
Z_BUFS = 4
STAGED_BUFS = 8


def load_scale_rows(queue, tile, rows, first):
    for r in range(4):
        queue.dma_start(out=tile[first + r : P : 32], in_=rows[r])


def tile_list_handle_patch_deform_kernel(
    tc, tab_words, tab_scales, tab2_words, tab2_scales, offs, offs2, qa, qb, hw, wd, w4_words, w4_scales, out
):
    nc = tc.nc
    with ExitStack() as ctx:
        keep = ctx.enter_context(tc.tile_pool(name="keep", bufs=1))
        ring = ctx.enter_context(tc.tile_pool(name="ring", bufs=RING_BUFS))
        shared = ctx.enter_context(tc.tile_pool(name="shared", bufs=1))
        psum = ctx.enter_context(tc.psum_pool(name="psum", bufs=PSUM_BUFS))

        list1 = keep.tile([P, S // 16], U16, name="list1")
        list2 = keep.tile([P, S2 // 16], U16, name="list2")
        tab_s = keep.tile([P, T // 4], I32, name="tab_s", align_bytes=64)
        tab2_s = keep.tile([P, T2 // 4], I32, name="tab2_s", align_bytes=64)
        qb_slot = shared.tile([P, 8, PACK], F32, name="qb_col", offset=24576 + 3072 - 64, align_bytes=64)
        qb_col = qb_slot[:, :BLOCKS, :]
        hw_col = keep.tile([P, PASSES, PACK], F32, name="hw_col", tag="after_hw", align_bytes=64)
        qa_col = keep.tile([P, PASSES, PACK], F32, name="qa_col", tag="after_qa", align_bytes=64)
        zeros = keep.tile([P, P], F32, name="zeros", tag="after_zeros", align_bytes=64)
        ident = keep.tile([P, P], F32, name="ident", tag="after_ident", align_bytes=64)
        one = keep.tile([P, 1], F32, name="one")
        root_of_one = keep.tile([P, 1], F32, name="root_of_one")

        nc.sync.dma_start(list1[:], offs)
        nc.sync.dma_start(out=hw_col[:], in_=hw.rearrange("(a p t) -> p a t", p=P, t=PACK))
        nc.sync.dma_start(out=qa_col[:], in_=qa.rearrange("(a p t) -> p a t", p=P, t=PACK))
        nc.gpsimd.memset(tab_s[:, T // 8 :], 0)
        nc.gpsimd.memset(zeros[:], 0.0)
        nc.vector.memset(tab_s[:, : T // 8], 0)
        nc.vector.memset(one[:], 1.0)
        nc.scalar.activation(root_of_one[:], one[:], ACT.Sqrt)
        nc.vector.memset(tab2_s[:], 0)
        nc.gpsimd.affine_select(
            out=ident[:],
            in_=zeros[:],
            compare_op=ALU.not_equal,
            fill=1.0,
            base=0,
            pattern=[[-1, P]],
            channel_multiplier=1,
        )
        nc.gpsimd.dma_start(out=qb_col, in_=qb.rearrange("(b p c) -> p b c", p=P, c=PACK))

        load_scale_rows(nc.sync, tab_s, tab_scales[0].bitcast(I32).rearrange("(q r) w -> r q w", r=4), 0)
        tab_w = keep.tile([P, T], I32, name="tab_w", tag="after_zeros", align_bytes=64)
        nc.sync.dma_start(out=tab_w[:], in_=tab_words[0].rearrange("p t i -> p (t i)").bitcast(I32))
        nc.sync.dma_start(list2[:], offs2)
        load_scale_rows(nc.sync, tab2_s, tab2_scales[0].bitcast(I32).rearrange("(q r) w -> r q w", r=4), TAB2_ROW)

        hw2 = keep.tile([P, PASSES, PACK], F32, name="hw2")
        hw2_qa = keep.tile([P, PASSES, PACK], F32, name="hw2_qa")
        hw2_qa_s = keep.tile([P, PASSES, PACK], F32, name="hw2_qa_s", tag="after_bases", align_bytes=64)
        nc.gpsimd.tensor_tensor(hw2[:], hw_col[:], hw_col[:], ALU.mult)
        nc.gpsimd.tensor_tensor(hw2_qa_s[:], hw2[:], qa_col[:], ALU.mult)
        nc.gpsimd.tensor_tensor(hw2_qa[:], hw2[:], qa_col[:], ALU.mult)
        tab2_w = keep.tile([P, T2], I32, name="tab2_w", tag="after_hw", align_bytes=64)
        nc.sync.dma_start(out=tab2_w[:], in_=tab2_words[0].rearrange("p t i -> p (t i)").bitcast(I32))

        qb_bank = {}
        for b in (1, 0, LAST):
            spread = psum.tile([P, PACK, P], F32, name=f"qb_bank{b}", tag=f"bank{4 + b}")
            for c in range(PACK):
                nc.tensor.transpose(spread[:, c, :], qb_col[:, b, c : c + 1].to_broadcast([P, P]), ident[:])
            qb_bank[b] = spread

        wd_raw0 = keep.tile([P, PACK, N], F32, name="wd_raw0", tag="after_qa", align_bytes=64)
        nc.sync.dma_start(out=wd_raw0[:], in_=wd[: P * PACK, :].rearrange("(p t) n -> p t n", t=PACK))
        wd_raw1 = []
        for h in range(2):
            half = shared.tile([P, PACK, N // 2], F32, name=f"wd_raw1{h}", offset=24576 + 3072 * h, align_bytes=64)
            rows = wd[P * PACK :, h * N // 2 : (h + 1) * N // 2]
            nc.sync.dma_start(out=half[:], in_=rows.rearrange("(p t) n -> p t n", t=PACK))
            wd_raw1.append(half)
        w4_s = keep.tile([P, PASSES, M // 4], I32, name="w4_s", tag="after_ident", align_bytes=64)
        nc.gpsimd.memset(w4_s[:], 0)
        load_scale_rows(nc.sync, w4_s, w4_scales.bitcast(I32).rearrange("a (q r) w -> r q a w", r=4), 0)

        base, hand_w, hand_s, vert_w, vert_s = {}, {}, {}, {}, {}
        wd_bf, wd_w, wd_s = {}, {}, {}
        listed_w = {}
        square, z_bf, z_w, z_s, qb_row, prod = {}, {}, {}, {}, {}, {}

        def copy_qb_row(b):
            qb_row[b] = keep.tile([P, BANK], F32, name=f"qb_row{b}", align_bytes=64)
            nc.scalar.copy(qb_row[b][:].rearrange("p (n c) -> p n c", c=PACK), qb_bank[b][:].rearrange("p c n -> p n c"))

        def make_base(b, a, ts, on_gpsimd):
            for t in ts:
                tile = keep.tile([P, BANK], F32, name=f"base{b}{a}{t}", tag=f"base{b}{a}{t}", align_bytes=64)
                if on_gpsimd:
                    nc.gpsimd.tensor_scalar(
                        tile[:], qb_row[b][:], hw2[:, a, t : t + 1], hw2_qa[:, a, t : t + 1], ALU.mult, ALU.add
                    )
                else:
                    nc.scalar.activation(
                        tile[:].rearrange("p (n c) -> p n c", c=PACK),
                        qb_bank[b][:].rearrange("p c n -> p n c"),
                        ACT.Identity,
                        bias=hw2_qa_s[:, a, t : t + 1],
                        scale=hw2[:, a, t : t + 1],
                    )
                base[b, a, t] = tile

        def gather_handle_scales(a):
            entries = list1[:, a * LIST_COLS : (a + 1) * LIST_COLS]
            picked = keep.tile([P, P, PACK], U8, name=f"picked{a}", align_bytes=64)
            nc.vector.tensor_copy(picked[:].rearrange("p m t -> p (m t)"), tab_s[:].bitcast(U8).indirect(entries))
            hand_s[a] = keep.tile([P, PACK, P], U8, name=f"hand_s{a}", align_bytes=64)
            nc.vector.tensor_copy(hand_s[a][:], picked[:].rearrange("p m t -> p t m"))

        def gather_handle_words(a, slot):
            listed_w[a] = keep.tile([P, P, PACK], U32, name=f"listed_w{a}", align_bytes=64)
            entries = list1[:, a * LIST_COLS : (a + 1) * LIST_COLS]
            nc.vector.tensor_copy(listed_w[a][:].rearrange("p m t -> p (m t)"), tab_w[:].bitcast(U32).indirect(entries))

        def part_handle_words(a):
            hand_w[a] = keep.tile([P, PACK, P], U32, name=f"hand_w{a}", align_bytes=64)
            nc.vector.tensor_copy(
                hand_w[a][:].rearrange("p t (c i) -> p c t i", i=PACK),
                listed_w[a][:].rearrange("p (c i) t -> p c t i", i=PACK),
            )

        def gather_vertex_scales(b0, b1, slot):
            tile = keep.tile([P, (b1 - b0) * BANK], U8, name=f"vert_s{b0}", tag=slot, align_bytes=64)
            entries = list2[:, b0 * LIST_COLS : b1 * LIST_COLS]
            nc.vector.tensor_copy(tile[:], tab2_s[:].bitcast(U8).indirect(entries))
            for b in range(b0, b1):
                vert_s[b] = tile[:, (b - b0) * BANK : (b - b0 + 1) * BANK]

        def gather_vertex_words(b, slot, at=None):
            if at is None:
                vert_w[b] = keep.tile([P, BANK], U32, name=f"vert_w{b}", tag=slot, align_bytes=64)
            else:
                vert_w[b] = shared.tile([P, BANK], U32, name=f"vert_w{b}", offset=at, align_bytes=64)
            entries = list2[:, b * LIST_COLS : (b + 1) * LIST_COLS]
            nc.vector.tensor_copy(vert_w[b][:], tab2_w[:].bitcast(U32).indirect(entries))

        def round_wd(a):
            wd_bf[a] = keep.tile([P, N, PACK], BF16, name=f"wd_bf{a}", align_bytes=64)
            for h in range(2):
                cols = slice(h * N // 2, (h + 1) * N // 2)
                if a == 0:
                    raw = wd_raw0[:, :, cols].rearrange("p t n -> p n t")
                    nc.gpsimd.tensor_scalar(wd_bf[a][:, cols, :], raw, 1.0, 0.0, ALU.mult, ALU.add)
                else:
                    nc.scalar.copy(
                        wd_bf[a][:, cols, :].rearrange("p (c i) t -> p c t i", i=LINE),
                        wd_raw1[h][:].rearrange("p t (c i) -> p c t i", i=LINE),
                    )

        def quantize_wd(a, slot):
            wd_w[a] = keep.tile([P, N], U32, name=f"wd_w{a}", align_bytes=64)
            wd_s[a] = keep.tile([P, N], U8, name=f"wd_s{a}", tag=slot, align_bytes=64)
            for c0, c1 in ((0, HALF), (HALF, N)):
                nc.vector.quantize_mx(
                    out=wd_w[a][:, c0:c1].bitcast(FP8X4),
                    scales=wd_s[a][:, c0:c1],
                    in_=wd_bf[a][:, c0:c1, :].rearrange("p n t -> p (n t)"),
                )

        def squares(b, a, c0, width, banks, at=None):
            if at is None:
                square[b, a, c0] = ring.tile([P, PACK, width], F32, name="square", bufs=SQUARE_BUFS)
            else:
                square[b, a, c0] = shared.tile([P, PACK, width], F32, name=f"square{b}{a}{c0}", offset=at, align_bytes=64)
            per_bank = BANK // width
            cols = slice(c0, c0 + width)
            for t0, bank in zip(range(0, PACK, per_bank), banks):
                dots = psum.tile([P, per_bank, width], F32, name="dots", tag=f"bank{bank}")
                for g in range(per_bank):
                    nc.tensor.matmul_mx(
                        out=dots[:, g, :],
                        lhsT=hand_w[a][:, t0 + g, :].bitcast(FP8X4),
                        lhsT_scale=hand_s[a][:, t0 + g, :],
                        rhs=vert_w[b][:, cols].bitcast(FP8X4),
                        rhs_scale=vert_s[b][TAB2_ROW:P, cols],
                        start=True,
                        stop=True,
                    )
                for g in range(per_bank):
                    t = t0 + g
                    nc.vector.scalar_tensor_tensor(
                        square[b, a, c0][:, t, :],
                        dots[:, g, :],
                        hw2_m2[:, a, t : t + 1],
                        base[b, a, t][:, cols],
                        ALU.mult,
                        ALU.add,
                    )

        def roots(b, a, c0, width, at=None):
            if at is None:
                z_bf[b, a, c0] = ring.tile([P, width, PACK], BF16, name="z_bf", align_bytes=64, bufs=ROUNDED_BUFS)
            else:
                z_bf[b, a, c0] = shared.tile([P, width, PACK], BF16, name=f"z_bf{b}{a}{c0}", offset=at, align_bytes=64)
            s0 = max(c for (bb, aa, c) in square if (bb, aa) == (b, a) and c <= c0)
            nc.scalar.activation(
                z_bf[b, a, c0][:].rearrange("p (c i) t -> p c t i", i=LINE),
                square[b, a, s0][:, :, c0 - s0 : c0 - s0 + width].rearrange("p t (c i) -> p c t i", i=LINE),
                ACT.Sqrt,
            )

        def quantize_z(b, a, c0, width):
            if c0 == 0:
                z_w[b, a] = ring.tile([P, BANK], U32, name="z_w", align_bytes=64, bufs=Z_BUFS)
                z_s[b, a] = ring.tile([P, BANK], U8, name="z_s", align_bytes=64, bufs=Z_BUFS)
            cols = slice(c0, c0 + width)
            nc.vector.quantize_mx(
                out=z_w[b, a][:, cols].bitcast(FP8X4),
                scales=z_s[b, a][:, cols],
                in_=z_bf[b, a, c0][:].rearrange("p j t -> p (j t)"),
            )

        def tiles_per_bank(width):
            return min(BANK // width, WD_TILES)

        def multiply(b, a, first, width, tile0, into=None, part=None):
            count = tiles_per_bank(width)
            if a == 0:
                prod[b, first, tile0] = psum.tile([P, count, width], F32, name="prod", tag=f"bank{into}")
            bank = prod[b, first, tile0]
            for g in range(count):
                row_tile = tile0 + g
                lo, hi = (0, width) if part is None else part
                step = hi - lo if (row_tile < WD_TILES or width == BANK) else P
                for c0 in range(lo, hi, step):
                    cols = slice(first + c0, first + c0 + step)
                    if row_tile < WD_TILES:
                        picked_rows = slice(row_tile * P, (row_tile + 1) * P)
                        weights = wd_w[a][:, picked_rows].bitcast(FP8X4)
                        weight_scales = wd_s[a][:, picked_rows]
                    else:
                        m = row_tile - WD_TILES
                        weights = w4_w[:, a, m * P // 2 : (m + 1) * P // 2].bitcast(U8).bitcast(FP4X4)
                        weight_scales = w4_s[:, a, m * P // 4 : (m + 1) * P // 4].bitcast(U8)
                    nc.tensor.matmul_mx(
                        out=bank[:, g, c0 : c0 + step],
                        lhsT=weights,
                        lhsT_scale=weight_scales,
                        rhs=z_w[b, a][:, cols].bitcast(FP8X4),
                        rhs_scale=z_s[b, a][:, cols],
                        start=(a == 0 and g == 0 and c0 == 0),
                        stop=(a == PASSES - 1 and g == count - 1 and c0 + step == width),
                    )

        def store(b, first, width, tile0, on_vector):
            count = tiles_per_bank(width)
            staged = ring.tile([P, count, width], F32, name="staged", bufs=STAGED_BUFS)
            if on_vector:
                nc.vector.tensor_copy(staged[:], prod[b, first, tile0][:])
            else:
                nc.scalar.copy(staged[:], prod[b, first, tile0][:])
            j0 = b * BANK + first
            nc.sync.dma_start(
                out=out[tile0 * P : (tile0 + count) * P, j0 : j0 + width].rearrange("(g p) j -> p g j", p=P),
                in_=staged[:],
            )

        def displace(b, first, width, tile0, on_vector):
            for a in range(PASSES):
                multiply(b, a, first, width, tile0)
            store(b, first, width, tile0, on_vector)

        copy_qb_row(1)
        copy_qb_row(LAST)
        make_base(1, 1, range(PACK), True)
        make_base(LAST, 0, range(PACK), True)
        make_base(LAST, 1, (3,), True)
        round_wd(0)
        w4_w = keep.tile([P, PASSES, M // 2], I32, name="w4_w", tag="qb_row1", align_bytes=64)
        nc.sync.dma_start(out=w4_w[:], in_=w4_words.bitcast(I32).rearrange("a p w -> p a w"))
        make_base(0, 0, range(PACK), False)
        make_base(0, 1, range(PACK), False)
        make_base(1, 0, range(PACK), False)
        make_base(LAST, 1, (0, 1), False)
        hw2_m2 = keep.tile([P, PASSES, PACK], F32, name="hw2_m2")
        nc.scalar.activation(hw2_m2[:], hw2[:], ACT.Copy, scale=-2.0)
        make_base(LAST, 1, (2,), False)
        round_wd(1)
        gather_handle_scales(0)
        gather_handle_scales(1)
        gather_vertex_scales(0, BLOCKS, "vert_s0")
        gather_handle_words(0, "hand_w0")
        gather_handle_words(1, "hand_w1")
        part_handle_words(0)
        part_handle_words(1)
        gather_vertex_words(0, "vert_w0")
        gather_vertex_words(1, "vert_w1")
        squares(0, 0, 0, BANK, (0, 1, 2, 3,))
        roots(0, 0, 0, BANK, 24576)
        squares(0, 1, 0, BANK, (0, 1, 2, 3,))
        roots(0, 1, 0, BANK, 4096)
        squares(1, 0, 0, BANK, (0, 1, 2, 3,))
        quantize_z(0, 0, 0, BANK)
        quantize_z(0, 1, 0, BANK)
        squares(1, 1, 0, BANK, (0, 1, 2, 3,), 7168)
        roots(1, 0, 0, BANK)
        multiply(0, 0, 0, BANK, 3, 4)
        multiply(0, 1, 0, BANK, 3)
        multiply(0, 0, 0, BANK, 4, 5)
        multiply(0, 1, 0, BANK, 4)
        multiply(0, 0, 0, BANK, 5, 6)
        multiply(0, 1, 0, BANK, 5)
        quantize_wd(0, "base110")
        quantize_wd(1, "base111")
        multiply(0, 0, 0, BANK, 0, 7)
        multiply(0, 1, 0, BANK, 0)
        quantize_z(1, 0, 0, BANK)
        store(0, 0, BANK, 3, False)
        multiply(0, 0, 0, BANK, 1, 4)
        multiply(0, 1, 0, BANK, 1)
        store(0, 0, BANK, 4, False)
        multiply(0, 0, 0, BANK, 2, 5)
        multiply(0, 1, 0, BANK, 2)
        store(0, 0, BANK, 5, False)
        roots(1, 1, 0, BANK, 16384)
        gather_vertex_words(2, "base112")
        multiply(1, 0, 0, BANK, 0, 0)
        multiply(1, 0, 0, BANK, 1, 1)
        multiply(1, 0, 0, BANK, 2, 2)
        multiply(1, 0, 0, BANK, 3, 3)
        store(0, 0, BANK, 0, False)
        store(0, 0, BANK, 1, False)
        store(0, 0, BANK, 2, False)
        quantize_z(1, 1, 0, BANK)
        squares(2, 0, 0, HALF, (6, 7,), 14336)
        multiply(1, 1, 0, BANK, 0)
        multiply(1, 1, 0, BANK, 1)
        squares(2, 1, 0, HALF, (4, 5,), 18432)
        multiply(1, 1, 0, BANK, 2)
        multiply(1, 1, 0, BANK, 3)
        store(1, 0, BANK, 0, False)
        store(1, 0, BANK, 1, False)
        roots(2, 0, 0, HALF)
        squares(2, 0, HALF, HALF, (6, 7,))
        multiply(1, 0, 0, BANK, 4, 0)
        multiply(1, 1, 0, BANK, 4)
        multiply(1, 0, 0, BANK, 5, 1)
        multiply(1, 1, 0, BANK, 5)
        store(1, 0, BANK, 2, False)
        roots(2, 1, 0, HALF)
        quantize_z(2, 0, 0, HALF)
        store(1, 0, BANK, 3, True)
        quantize_z(2, 1, 0, HALF)
        squares(2, 1, HALF, HALF, (4, 5,))
        roots(2, 0, HALF, HALF)
        store(1, 0, BANK, 4, False)
        quantize_z(2, 0, HALF, HALF)
        multiply(2, 0, 0, HALF, 0, 2)
        multiply(2, 1, 0, HALF, 0)
        multiply(2, 0, 0, HALF, 2, 3)
        multiply(2, 1, 0, HALF, 2)
        multiply(2, 0, 0, HALF, 4, 6)
        multiply(2, 1, 0, HALF, 4)
        roots(2, 1, HALF, P)
        roots(2, 1, HALF + P, P)
        store(1, 0, BANK, 5, True)
        quantize_z(2, 1, HALF, P)
        multiply(2, 0, HALF, P, 0, 7)
        multiply(2, 0, HALF, P, 3, 4)
        multiply(2, 1, HALF, P, 0)
        multiply(2, 1, HALF, P, 3)
        multiply(2, 0, HALF + P, P, 0, 5)
        multiply(2, 0, HALF + P, P, 3, 0)
        store(2, 0, HALF, 0, True)
        quantize_z(2, 1, HALF + P, P)
        store(2, 0, HALF, 2, False)
        multiply(2, 1, HALF + P, P, 0)
        multiply(2, 1, HALF + P, P, 3)
        store(2, 0, HALF, 4, False)
        store(2, HALF, P, 0, True)
        store(2, HALF, P, 3, False)
        store(2, HALF + P, P, 0, True)
        store(2, HALF + P, P, 3, False)
